import numpy as np, ml_dtypes
CORES = [16,18,20,22]
N = 4
BF = ml_dtypes.bfloat16
def gentries(a):
    return np.ascontiguousarray(a.reshape(8, 16, -1).transpose(0, 2, 1)).reshape(8, -1)
def gtable(e):
    e = np.asarray(e); return np.ascontiguousarray(e.reshape(8, -1, 16).transpose(0, 2, 1)).reshape(128, -1).astype(np.int32)
M, D, L, Q = 4096, 4, 4, 2048
S = [0, 4096, 6144, 7168, 7680, 7936]
NODES = S[-1]; FULL = 2 ** L - 1; QP = Q // N
def gtables(a):
    return np.stack([gtable(e) for e in a])
def letters(rng, *shape):
    return np.left_shift(np.uint8(1), rng.integers(0, L, shape, dtype=np.uint8))
def anyset(rng, *shape):
    return rng.integers(1, FULL + 1, shape, dtype=np.uint8)
def tobf(v):
    return v.astype(np.float32).astype(BF)
def pairs(rng):
    le = np.zeros((N, 8, NODES - M), np.int64); ri = le.copy()
    for d in range(1, D + 1):
        e = S[d - 1] + np.argsort(rng.random((N, 8, S[d] - S[d - 1])), axis=2); a, b = S[d] - M, S[d + 1] - M
        le[:, :, a:b] = e[:, :, 0::2]; ri[:, :, a:b] = e[:, :, 1::2]
    return le, ri
def nodes(rng):
    d = rng.integers(0, D + 1, (N, 8, Q)); lo = np.array(S)[d]; n = np.array(S)[d + 1] - lo
    return lo + np.minimum((rng.random((N, 8, Q)) * n).astype(np.int64), n - 1)
def setup_inputs(rng):
    le, ri = pairs(rng)
    leaf = np.where(rng.random((N, 128, M), dtype=np.float32) < 0.125, anyset(rng, N, 128, M), letters(rng, N, 128, M))
    return {"leaf": tobf(leaf), "left": gtables(le), "right": gtables(ri), "clade": gtables(nodes(rng)), "edge": gtables(nodes(rng))}
def setup_inputs_near(rng):
    d = setup_inputs(rng); rate = np.repeat(0.1 * (1 + np.arange(8)), 16).reshape(1, 128, 1).astype(np.float32)
    leaf = np.where(rng.random((N, 128, M), dtype=np.float32) < rate, d["leaf"].astype(np.float32), letters(rng, 1, 128, 1).astype(np.float32))
    d["leaf"] = tobf(leaf); return d
def setup_inputs_order(rng):
    d = setup_inputs(rng); le = np.zeros((N, 8, NODES - M), np.int64); ri = le.copy()
    for k in range(1, D + 1):
        e = np.arange(S[k - 1], S[k]); a, b = S[k] - M, S[k + 1] - M
        le[0::2, :, a:b] = e[0::2]; ri[0::2, :, a:b] = e[1::2]
        le[1::2, :, a:b] = e[::-1][0::2]; ri[1::2, :, a:b] = e[::-1][1::2]
    d["left"] = gtables(le); d["right"] = gtables(ri)
    j = np.broadcast_to(np.arange(Q), (N, 8, Q))
    d["edge"] = gtables(j); d["clade"] = gtables(NODES - 1 - j); return d
def setup_inputs_few(rng):
    d = setup_inputs(rng); p = np.array([0, M - 1, M, S[D], NODES - 1])
    d["clade"] = gtables(p[rng.integers(0, 5, (N, 8, Q))]); d["edge"] = gtables(p[rng.integers(0, 5, (N, 8, Q))]); return d
def setup_inputs_far(rng):
    d = setup_inputs_order(rng); h = M // 2
    a = rng.integers(0, L, (1, 128, 1)); b = (a + rng.integers(1, L, (1, 128, 1))) % L
    leaf = np.where(np.arange(M) < h, np.left_shift(1, a), np.left_shift(1, b))
    d["leaf"] = tobf(np.repeat(leaf, N, axis=0))
    c = rng.integers(h, M, (N, 8, Q)); mv = (rng.random((N, 8, Q)) < 0.125) & (np.arange(8).reshape(1, 8, 1) >= 4)
    d["clade"] = gtables(np.where(mv, c - h, c)); d["edge"] = gtables(rng.integers(0, h, (N, 8, Q))); return d
def setup_inputs_spread(rng):
    d = setup_inputs(rng); p = rng.random((N, 128, L)) ** 3 + 1e-6; c = np.add.accumulate(p, axis=2); c = (c / c[:, :, -1:]).astype(np.float32)
    x = rng.random((N, 128, M), dtype=np.float32); lt = np.zeros((N, 128, M), np.uint8)
    for k in range(L - 1): lt += x > c[:, :, k:k + 1]
    am = rng.choice(np.array([0, 0, 0, 0.02, 0.02, 1], np.float32), (N, 1, M))
    amb = np.where(rng.random((N, 128, M), dtype=np.float32) < 0.5, np.uint8(FULL), anyset(rng, N, 128, M))
    d["leaf"] = tobf(np.where(rng.random((N, 128, M), dtype=np.float32) < am, amb, np.left_shift(np.uint8(1), lt)))
    e = np.minimum((NODES * rng.random((N, 8, Q)) ** 4).astype(np.int64), NODES - 1); h = np.minimum((NODES * rng.random((N, 8, Q)) ** 4).astype(np.int64), NODES - 1)
    d["edge"] = gtables(e); d["clade"] = gtables(NODES - 1 - h); return d
def check_inputs(d):
    bad = []
    try:
        v = d["leaf"].astype(np.float32)
        if not ((v == np.floor(v)) & (v >= 1) & (v <= FULL)).all(): bad.append("leaf")
        ok = True
        for q in range(N):
            le, ri = gentries(d["left"][q]), gentries(d["right"][q])
            for k in range(1, D + 1):
                a, b = S[k] - M, S[k + 1] - M
                e = np.sort(np.concatenate([le[:, a:b], ri[:, a:b]], axis=1), axis=1)
                ok = ok and bool((e == np.arange(S[k - 1], S[k])).all())
        if not ok: bad.append("left and right")
        for a in ("clade", "edge"):
            if not ((d[a] >= 0) & (d[a] < NODES)).all(): bad.append(a)
    except Exception:
        bad.append("shapes")
    return bad
def fitch(a, b):
    i = a & b
    return np.where(i > 0, i, a | b)
def reference(leaf, left, right, clade, edge):
    inside = np.zeros((N, 8, 16, NODES), np.uint8); outside = np.full((N, 8, 16, NODES), FULL, np.uint8)
    inside[:, :, :, :M] = leaf.astype(np.float32).astype(np.uint8).reshape(N, 8, 16, M)
    for q in range(N):
        le, ri = gentries(left[q]), gentries(right[q])
        for g in range(8):
            u, o = inside[q, g], outside[q, g]
            for d in range(1, D + 1):
                x, z = le[g, S[d] - M:S[d + 1] - M], ri[g, S[d] - M:S[d + 1] - M]
                u[:, S[d]:S[d + 1]] = fitch(u[:, x], u[:, z])
            for d in range(D, 0, -1):
                x, z = le[g, S[d] - M:S[d + 1] - M], ri[g, S[d] - M:S[d + 1] - M]
                o[:, x] = fitch(o[:, S[d]:S[d + 1]], u[:, z])
                o[:, z] = fitch(o[:, S[d]:S[d + 1]], u[:, x])
    on = fitch(inside, outside); c = np.zeros((N, 8, Q), np.int64)
    for r in range(N):
        cl, ed = gentries(clade[r]), gentries(edge[r])
        for g in range(8):
            for q in range(N):
                j = slice(q * QP, (q + 1) * QP)
                c[r, g, j] = np.sum((inside[q, g][:, cl[g, j]] & on[r, g][:, ed[g, j]]) == 0, axis=0)
    runs = c.reshape(N, 8, 8, Q // 8)
    return {"cost": np.min(runs, axis=2).astype(np.float32), "first": np.argmin(runs, axis=2).astype(np.float32)}

@@ -1,0 +1,377 @@
+from concourse.bass import DstId, RemoteDMATransfer
+from concourse.mybir import AluOpType as OP, ActivationFunctionType as AF
+
+S = [0, 4096, 6144, 7168, 7680, 7936]
+NT = 12
+PB = 14
+CHUNK = {1: 512, 2: 256, 3: 256, 4: 128}
+GA, SC = 1.56, 3.8
+
+BUFS = {
+    "bfloat16": {"raw": 4096, "f2": 4096, "f4": 4096, "f8": 4096, "win": 7936, "outl": 7936, "ca": 3840, "cb": 3840, "top": 512,
+                 "orb": 3072, "oo": 3584, "tY": 256 * NT, "tB": 256 * NT, "tH": 256 * NT, "uh": 256 * NT, "ul": 256 * NT,
+                 "ole": 2048, "ore": 2048, "ine": 2048, "zz": 2048, "land": 2048, "clout": 2048, "one": 128, "gsum": 192},
+    "float32": {"outr": 7936, "pre": 2048, "key": 64 * 17, "res": 128},
+    "int32": {"tS": 256 * NT, "tT": 256 * NT, "li": 240, "ri": 240, "ci": 128, "ei": 128, "keyi": 192},
+    "uint16": {"lo": 240, "ro": 240, "cu": 128, "cin": 128, "eu": 128},
+}
+DIAG = {"i1": 1.0, "i2": 2.0, "i8": 8.0, "i32": 32.0, "ik": -256.0, "im": 2.0 ** -12, "ip": 2.0 ** -PB, "iq": 2.0 ** PB}
+SCRATCH = {}
+for _t in BUFS:
+    for _b in BUFS[_t]:
+        SCRATCH[_b] = ("sbuf", [32 if _b in ("key", "keyi", "res") else 128, BUFS[_t][_b]], _t)
+for _b in DIAG:
+    SCRATCH[_b] = ("sbuf", [128, 128], "bfloat16")
+for _b in range(8):
+    SCRATCH["ps%d" % _b] = ("psum", [128, 512], "float32")
+SEMAPHORES = (["qV", "qA", "qP", "qG", "snd"] + ["ld%d" % i for i in range(10)] + ["lst%d" % i for i in range(4)]
+              + ["clr%d" % i for i in range(4)])
+
+
+def rank_program(g, core, T, topo):
+    rank = T.rank_of(core)
+    if rank is None:
+        return
+    others = [q for q in range(len(T.cores)) if q != rank]
+    ops = []
+
+    def op(eng, fns, cost, R=(), W=(), lat=0.0, dma=None, inc=0, seen=None):
+        ops.append({"eng": eng, "fns": fns, "cost": cost, "R": list(R), "W": list(W), "lat": lat, "dma": dma, "inc": inc, "seen": seen})
+
+    def V(fn, n, c, R, W):
+        op("V", [fn], 30 + 1.04 * max(64, n * c), R, W)
+
+    def A(fn, n, c, R, W):
+        op("A", [fn], 50 + 1.04 * n * c, R, W)
+
+    def P(fns, n, R, W):
+        op("P", fns, 40 + 0.5 * max(64, n) * len(fns), R, W)
+
+    def G(fn, n, R, W):
+        op("G", [fn], 150 + 2.08 * n, R, W)
+
+    bank, slots = [0], [0]
+
+    def newbank():
+        bank[0] += 1
+        return "ps%d" % ((bank[0] - 1) % 8)
+
+    def newslot():
+        slots[0] += 1
+        return 256 * ((slots[0] - 1) % NT)
+
+    def reg(b, a, n):
+        return (b, 0, 512) if b[:2] == "ps" else (b, a, a + n)
+
+    def mm(ps, terms, n, start=True, stop=True):
+        fns = []
+        for k, (m, b, a) in enumerate(terms):
+            st, sp = start and k == 0, stop and k == len(terms) - 1
+            fns.append(lambda m=m, b=b, a=a, st=st, sp=sp: g.tensor.matmul(T[ps][:, 0:n], T[m][:], T[b][:, a:a + n], st, sp))
+        P(fns, n, [(m, 0, 128) for m, b, a in terms] + [(b, a, a + n) for m, b, a in terms], [(ps, 0, 512)])
+
+    def ts(dst, d0, src, s0, n, c, s1=None, op0=None, s2=None, op1=None):
+        o, i = (lambda: T[dst][:, d0:d0 + n]), (lambda: T[src][:, s0:s0 + n])
+        if op0 is None:
+            fn = lambda: g.vector.tensor_copy(o(), i())
+        elif op1 is None:
+            fn = lambda: g.vector.tensor_scalar(o(), i(), s1, None, op0)
+        else:
+            fn = lambda: g.vector.tensor_scalar(o(), i(), s1, s2, op0, op1)
+        V(fn, n, c, [reg(src, s0, n)], [reg(dst, d0, n)])
+
+    def tt(dst, d0, x, x0, y, y0, n, c, o):
+        V(lambda: g.vector.tensor_tensor(T[dst][:, d0:d0 + n], T[x][:, x0:x0 + n], T[y][:, y0:y0 + n], o), n, c,
+          [reg(x, x0, n), reg(y, y0, n)], [reg(dst, d0, n)])
+
+    def act(dst, d0, src, s0, n, func=AF.Copy, scale=1.0, bias=0.0):
+        A(lambda: g.scalar.activation(T[dst][:, d0:d0 + n], T[src][:, s0:s0 + n], func, bias=bias, scale=scale), n, 1,
+          [reg(src, s0, n)], [reg(dst, d0, n)])
+
+    def single(terms, n, dst, d0):
+        ps, pw, o = newbank(), newbank(), newslot()
+        mm(ps, terms, n)
+        mm(pw, terms, n, stop=False)
+        ts("tS", o, ps, 0, n, 1)
+        ts("tT", o, "tS", o, n, 1, 1, OP.logical_shift_right, 0x55, OP.bitwise_and)
+        ts("tB", o, "tT", o, n, 1)
+        mm(pw, [("ik", "tB", o)], n, start=False)
+        tt(dst, d0, "tB", o, pw, 0, n, 1, OP.max)
+
+    def pair(lo, hi, n):
+        pp, ph, pl, o = newbank(), newbank(), newbank(), newslot()
+        mm(pp, [("i1", b, a) for b, a in hi] + [("ip", b, a) for b, a in lo], n)
+        mm(ph, [("i1", b, a) for b, a in hi], n, stop=False)
+        mm(pl, [("i1", b, a) for b, a in lo], n, stop=False)
+        ts("tS", o, pp, 0, n, 1, 2.0 ** PB, OP.mult, float(2 ** (PB + 8)), OP.add)
+        ts("tT", o, "tS", o, n, 1, 1, OP.logical_shift_right, 0x55 + (0x55 << PB) + (1 << PB + 7), OP.bitwise_and)
+        ts("tY", o, "tT", o, n, 1, 2.0 ** -PB, OP.mult)
+        mm(pp, [("iq", "tY", o)], n)
+        tt("tB", o, "tT", o, pp, 0, n, 1, OP.subtract)
+        ts("tH", o, "tY", o, n, .5, -128.0, OP.add)
+        mm(ph, [("ik", "tH", o)], n, start=False)
+        mm(pl, [("ik", "tB", o)], n, start=False)
+        return ph, pl, o
+
+    def double(terms_of, n, dst, d0):
+        ph, pl, o = pair(terms_of(0), terms_of(n), n)
+        tt(dst, d0 + n, "tH", o, ph, 0, n, 1, OP.max)
+        tt(dst, d0, "tB", o, pl, 0, n, 1, OP.max)
+
+    def gather(eng, dst, d0, src, a, b, off, c0, n, scale=1.0):
+        ind = lambda: T[src][:, a:b].indirect(T[off][:, c0:c0 + n // 16])
+        R, W = [(src, a, b), (off, c0, c0 + n // 16)], [(dst, d0, d0 + n)]
+        if eng == "V":
+            V(lambda: g.vector.tensor_copy(T[dst][:, d0:d0 + n], ind()), n, GA, R, W)
+        else:
+            A(lambda: g.scalar.activation(T[dst][:, d0:d0 + n], ind(), AF.Copy, scale=scale), n, GA, R, W)
+
+    def load(eng, i, dst, a, b, src, lat):
+        q = g.sync if eng == "Y" else g.scalar
+        op(eng, [lambda: q.dma_start(T[dst][:, a:b], T[src][:, a:b])], 120, [], [(dst, a, b)], lat=lat, dma="ld%d" % i, inc=16)
+
+    for k in range(4):
+        load("Y", k, "raw", 1024 * k, 1024 * k + 1024, "leaf", 2000 + 800 * k)
+    load("A", 4, "ci", 0, 128, "clade", 2200)
+    load("A", 5, "li", 0, 240, "left", 2600)
+    load("A", 6, "ri", 0, 240, "right", 3000)
+    load("Y", 7, "ei", 0, 128, "edge", 6500)
+
+    V(lambda: g.vector.memset(T.one[:], 1.0), 128, .5, [], [("one", 0, 128)])
+    G(lambda: g.affine_select(T.i1[:], T.one[:], [[-1, 128]], OP.is_equal, 0.0, 0, 1), 128, [("one", 0, 128)], [("i1", 0, 128)])
+    for nm in DIAG:
+        if nm != "i1":
+            ts(nm, 0, "i1", 0, 128, .5, DIAG[nm], OP.mult)
+
+    ts("cu", 0, "ci", 0, 128, 1)
+    for d in range(1, 5):
+        c0, c1 = (S[d] - 4096) // 16, (S[d + 1] - 4096) // 16
+        for x, y in (("li", "lo"), ("ri", "ro")):
+            ts(y, c0, x, c0, c1 - c0, 1, float(-S[d - 1]), OP.add)
+
+    def fused(src, dst, w, sem):
+        tr = []
+        for i, q in enumerate(others):
+            to = T.cores[q]
+            rid, pid, _e = topo.addr(to)
+            en = topo.engines(core, to)[4 * i:4 * i + 4]
+            tr.append(RemoteDMATransfer(dst_ids=[DstId(rid=rid, pnc=pid)], dma_engine_mask=sum(1 << e for e in en),
+                                        remote_sem=T.sem[sem + str(rank)], src=T[src][:, w * q:w * q + w],
+                                        dst=T[dst][:, w * rank:w * rank + w]))
+        g.remote_dma_fused(tr, local_sem=T.sem.snd)
+        return None
+
+    def exchange(src, dst, w, sem, t):
+        op("G", [lambda: fused(src, dst, w, sem)], 1500, [(src, w * q, w * q + w) for q in others], [], lat=2000, dma="snd", inc=12)
+        for q in others:
+            op(None, [], t, [], [(dst, w * q, w * q + w)], seen=(sem + str(q), 4))
+
+    exchange("cu", "cin", 32, "lst", 6000)
+    ts("eu", 0, "ei", 0, 128, 1)
+
+    for a in range(0, 4096, 512):
+        for nm, m, c in (("f2", .5, 129 - .25), ("f4", .25, 129 - .375), ("f8", .125, 129 - .4375)):
+            if nm == "f8" and a < 1536:
+                act(nm, a, "raw", a, 512, AF.Copy, m, c)
+            else:
+                ts(nm, a, "raw", a, 512, .5, m, OP.mult, c, OP.add)
+        ps = newbank()
+        mm(ps, [("i1", "raw", a), ("i2", "f2", a), ("i8", "f4", a), ("i32", "f8", a)], 512)
+        act("win", a, ps, 0, 512, AF.Copy, 1.0, -129.0 * 42)
+
+    def zero(buf, a, b):
+        G(lambda: g.iota(T[buf][:, a:b], [[0, b - a]], 0, 0, allow_small_or_imprecise_dtypes=True), b - a, [("i1", 0, 128)], [(buf, a, b)])
+
+    V(lambda: g.vector.memset(T.outl[:, S[4]:S[5]], 85.0), 256, .5, [], [("outl", S[4], S[5])])
+    for d in (2, 1):
+        zero("outl", S[d], S[d + 1])
+        zero("outr", S[d], S[d + 1])
+    zero("outr", S[3], S[5])
+
+    for d in range(1, 5):
+        base, nn, n = S[d] - 4096, S[d + 1] - S[d], CHUNK[d]
+        for a in range(0, nn, n):
+            c = base + a
+            gather("A", "ca", c, "win", S[d - 1], S[d], "lo", c // 16, n)
+            gather("V" if a == 0 else "A", "cb", c, "win", S[d - 1], S[d], "ro", c // 16, n)
+            if d < 3:
+                double(lambda e, c=c: [("ca", c + e), ("cb", c + e)], n // 2, "win", S[d] + a)
+            else:
+                single([("i1", "ca", c), ("i1", "cb", c)], n, "win", S[d] + a)
+
+    for k, x, y in ((0, "cb", "lo"), (256, "ca", "ro")):
+        ts("top", k, x, 3584, 256, .5, 85.0, OP.add)
+        V(lambda k=k, y=y: g.vector.tensor_copy(T.outl[:, S[3]:S[4]].indirect(T[y][:, 224:240]), T.top[:, k:k + 256]), 256, SC,
+          [("top", k, k + 256), (y, 224, 240)], [("outl", S[3], S[4])])
+    ts("oo", 3072, "outl", S[3], 512, .5, -85.0, OP.add)
+
+    for q in others + [rank]:
+        dst, off = ("land", "cu") if q == rank else ("clout", "cin")
+        gather("A", dst, 512 * q, "win", 0, S[5], off, 32 * q, 512)
+    exchange("clout", "land", 512, "clr", 35000)
+    for a in (0, 2048):
+        zero("outl", a, a + 2048)
+        zero("outr", a, a + 2048)
+    for a in range(0, 2048, 512):
+        gather("A", "ine", a, "win", 0, S[5], "eu", a // 16, 512)
+
+    for d in (3, 2, 1):
+        base, nn = S[d] - 4096, S[d + 1] - S[d]
+        n = 256 if d == 3 else 512
+        lo_, hi_ = S[d - 1], S[d]
+        for a in range(0, nn, n):
+            c, w = base + a, S[d] + a
+            if d < 3:
+                act("orb", c, "outr", w, n, AF.Copy, 4096.0)
+                for z in (0, 256):
+                    double(lambda e, c=c + z, w=w + z: [("outl", w + e), ("orb", c + e)], 128, "oo", c + z)
+            V(lambda c=c, n=n, lo_=lo_, hi_=hi_: g.vector.tensor_tensor(
+                T.outl[:, lo_:hi_].indirect(T.lo[:, c // 16:(c + n) // 16]), T.oo[:, c:c + n], T.cb[:, c:c + n], OP.add), n, SC,
+              [("oo", c, c + n), ("cb", c, c + n), ("lo", c // 16, (c + n) // 16)], [("outl", lo_, hi_)])
+            ps, p = newbank(), c % 2048
+            mm(ps, [("im", "oo", c), ("im", "ca", c)], n)
+            act("pre", p, ps, 0, n)
+            A(lambda p=p, c=c, n=n, lo_=lo_, hi_=hi_: g.scalar.activation(
+                T.outr[:, lo_:hi_].indirect(T.ro[:, c // 16:(c + n) // 16]), T.pre[:, p:p + n], AF.Tanh), n, SC,
+              [("pre", p, p + n), ("ro", c // 16, (c + n) // 16)], [("outr", lo_, hi_)])
+
+    def sel(d0, s0, src, pat, o, base, cm):
+        G(lambda: g.affine_select(T.gsum[:, d0:d0 + 32], T[src][:, s0:s0 + 32], pat, o, 0.0, base, cm), 32, [reg(src, s0, 32)], [("gsum", d0, d0 + 32)])
+
+    sel(128, 0, "one", [[-16, 8], [0, 4]], OP.is_ge, 0, 1)
+    sel(160, 128, "gsum", [[16, 8], [0, 4]], OP.is_ge, 15, -1)
+    ts("gsum", 128, "gsum", 160, 32, 1, 8.0, OP.mult)
+    for b in range(4):
+        sel(32 * b, 128, "gsum", [[0, 8], [1, 4]], OP.is_equal, -b, 0)
+
+    for a in range(0, 2048, 512):
+        gather("A", "ore", a, "outr", 0, S[5], "eu", a // 16, 512, scale=4096.0)
+        V(lambda a=a: g.vector.tensor_tensor(T.ole[:, a:a + 512], T.outl[:, 0:S[5]].indirect(T.eu[:, a // 16:a // 16 + 32]), T.ore[:, a:a + 512], OP.add), 512, GA,
+          [("outl", 0, S[5]), ("eu", a // 16, a // 16 + 32), ("ore", a, a + 512)], [("ole", a, a + 512)])
+    for a in range(0, 2048, 512):
+        n, h = 256, a + 256
+        ph, pl, o = pair([("ole", a)], [("ole", h)], n)
+        act("uh", o, ph, 0, n, AF.Relu)
+        act("ul", o, pl, 0, n, AF.Relu)
+        ph, pl, o2 = pair([("ine", a), ("tB", o), ("ul", o)], [("ine", h), ("tH", o), ("uh", o)], n)
+        act("uh", o2, ph, 0, n, AF.Relu)
+        act("ul", o2, pl, 0, n, AF.Relu)
+        pp, o = newbank(), newslot()
+        mm(pp, [("i1", "land", h), ("i1", "tH", o2), ("i1", "uh", o2), ("ip", "land", a), ("ip", "tB", o2), ("ip", "ul", o2)], n)
+        ts("tS", o, pp, 0, n, 1, 2.0 ** PB, OP.mult)
+        for m, z in ((0xAA << PB, h), (0xAA, a)):
+            o2 = newslot()
+            ts("tT", o2, "tS", o, n, 1, m, OP.bitwise_and)
+            ts("zz", z, "tT", o2, n, 1, 0.0, OP.is_equal)
+        ps = newbank()
+        fns = []
+        for kk in range(2):
+            for b in range(4):
+                fns.append(lambda kk=kk, b=b, ps=ps, a=a: g.tensor.matmul(
+                    T[ps][0:32, 64 * kk:64 * kk + 64], T.gsum[:, 32 * b:32 * b + 32],
+                    T.zz[:, a + 256 * kk + 64 * b:a + 256 * kk + 64 * b + 64], b == 0, b == 3))
+        P(fns, 64, [("gsum", 0, 128), ("zz", a, a + 512)], [(ps, 0, 512)])
+        for kk in range(2):
+            k = a // 256 + kk
+            c, r0 = 64 * k, 64 * (7 + k)
+            V(lambda ps=ps, kk=kk, k=k, c=c: g.vector.tensor_scalar(T.key[:, c:c + 64], T[ps][0:32, 64 * kk:64 * kk + 64], float(k), None, OP.add),
+              64, 1, [(ps, 0, 512)], [("key", c, c + 64)])
+            if k:
+                tt("key", r0 + 64, "key", 0 if k == 1 else r0, "key", c, 64, 2, OP.min)
+    ts("keyi", 0, "key", 960, 64, 1)
+    ts("keyi", 64, "keyi", 0, 64, 1, 3, OP.logical_shift_right)
+    ts("keyi", 128, "keyi", 0, 64, 1, 7, OP.bitwise_and)
+    ts("res", 0, "keyi", 64, 64, 1)
+    ts("res", 64, "keyi", 128, 64, 1)
+    op("Y", [lambda: g.sync.dma_start(T.cost[:], T.res[:, 0:64])], 120, [("res", 0, 64)], [], lat=2000, dma="ld8", inc=16)
+    op("Y", [lambda: g.sync.dma_start(T["first"][:], T.res[:, 64:128])], 120, [("res", 64, 128)], [], lat=2000, dma="ld9", inc=16)
+
+    run(g, T, ops)
+
+
+def run(g, T, ops):
+    n = len(ops)
+    deps = [dict() for _ in ops]
+    hist = {}
+    for i, o in enumerate(ops):
+        for kind, regs in (("R", o["R"]), ("W", o["W"])):
+            for r in regs:
+                psum = r[0][:2] == "ps"
+                for (a, b, j, w) in hist.get(r[0], ()):
+                    if j == i or not (a < r[2] and r[1] < b):
+                        continue
+                    same = ops[j]["eng"] == o["eng"]
+                    if not w and kind == "R" and (same or not psum):
+                        continue
+                    hard = (w and kind == "R") or not same or ops[j]["dma"] is not None or o["eng"] != "P"
+                    deps[i][j] = deps[i].get(j, False) or hard
+        for r in o["R"]:
+            hist.setdefault(r[0], []).append((r[1], r[2], i, False))
+        for r in o["W"]:
+            h = hist.get(r[0], [])
+            hist[r[0]] = [e for e in h if not (r[1] <= e[0] and e[1] <= r[2])] + [(r[1], r[2], i, True)]
+    succ = [[] for _ in ops]
+    for i in range(n):
+        for j in deps[i]:
+            succ[j].append(i)
+    tail = [0.0] * n
+    for i in range(n - 1, -1, -1):
+        tail[i] = ops[i]["cost"] + ops[i]["lat"] + max([tail[k] + 80 for k in succ[i]] or [0.0])
+    free, fin = {}, [0.0] * n
+    need = [len(d) for d in deps]
+    ready = [i for i in range(n) if not need[i]]
+    est = dict((i, 0.0) for i in ready)
+    order = []
+    while ready:
+        best = min(ready, key=lambda i: max(est[i], free.get(ops[i]["eng"], 0.0) if ops[i]["eng"] else 0.0))
+        e = ops[best]["eng"]
+        bt = max(est[best], free.get(e, 0.0) if e else 0.0)
+        if e:
+            cand = [i for i in ready if ops[i]["eng"] == e and max(est[i], free.get(e, 0.0)) <= bt + 300]
+            best = max(cand, key=lambda i: (tail[i], -i))
+            bt = max(est[best], free.get(e, 0.0))
+            free[e] = bt + ops[best]["cost"]
+        fin[best] = bt + ops[best]["cost"] + ops[best]["lat"]
+        order.append(best)
+        ready.remove(best)
+        for k in succ[best]:
+            need[k] -= 1
+            if not need[k]:
+                ready.append(k)
+                est[k] = max(fin[j] + 80 for j in deps[k])
+    queue = {"V": g.vector, "A": g.scalar, "P": g.tensor, "G": g, "Y": g.sync}
+    csem = {"V": "qV", "A": "qA", "P": "qP", "G": "qG"}
+    total, val = {}, [None] * n
+    clock = {e: {} for e in queue}
+    snap = [None] * n
+    for i in order:
+        o = ops[i]
+        e = o["eng"]
+        if e is None:
+            val[i], snap[i] = o["seen"], {}
+            total[o["seen"][0]] = o["seen"][1]
+            continue
+        ck = clock[e]
+        todo = sorted([j for j in deps[i] if deps[i][j]], key=lambda j: -fin[j])
+        for j in todo:
+            s = val[j][0]
+            if ck.get(s, 0) >= val[j][1]:
+                continue
+            same = [x for x in todo if val[x][0] == s]
+            v = max(val[x][1] for x in same)
+            queue[e].wait_ge(T.sem[s], v)
+            for x in same:
+                for k2, v2 in snap[x].items():
+                    ck[k2] = max(ck.get(k2, 0), v2)
+            ck[s] = max(ck.get(s, 0), v)
+        s = o["dma"] or csem[e]
+        for fn in o["fns"]:
+            ins = fn()
+            if ins is not None:
+                ins.then_inc(T.sem[s], o["inc"] or 1)
+            total[s] = total.get(s, 0) + (o["inc"] or 1)
+        val[i], snap[i] = (s, total[s]), dict(ck)
+    for s in sorted(total):
+        if clock["Y"].get(s, 0) < total[s]:
+            g.sync.wait_ge(T.sem[s], total[s])
+    return fin

@@ -98,7 +98,7 @@ def rank_program(g, core, T, topo):
         mm(pw, [("ik", "tB", o)], n, start=False)
         tt(dst, d0, "tB", o, pw, 0, n, 1, OP.max)
 
-    def pair(lo, hi, n):
+    def pair(lo, hi, n, th):
         pp, ph, pl, o = newbank(), newbank(), newbank(), newslot()
         mm(pp, [("i1", b, a) for b, a in hi] + [("ip", b, a) for b, a in lo], n)
         mm(ph, [("i1", b, a) for b, a in hi], n, stop=False)
@@ -108,15 +108,20 @@ def rank_program(g, core, T, topo):
         ts("tY", o, "tT", o, n, 1, 2.0 ** -PB, OP.mult)
         mm(pp, [("iq", "tY", o)], n)
         tt("tB", o, "tT", o, pp, 0, n, 1, OP.subtract)
-        ts("tH", o, "tY", o, n, .5, -128.0, OP.add)
-        mm(ph, [("ik", "tH", o)], n, start=False)
+        if th == "A":
+            act("tH", o, "tY", o, n, AF.Copy, 1.0, -128.0)
+        elif th == "V":
+            ts("tH", o, "tY", o, n, .5, -128.0, OP.add)
+        mm(ph, [("ik", "tH" if th else "tY", o)], n, start=False)
         mm(pl, [("ik", "tB", o)], n, start=False)
         return ph, pl, o
 
-    def double(terms_of, n, dst, d0):
-        ph, pl, o = pair(terms_of(0), terms_of(n), n)
-        tt(dst, d0 + n, "tH", o, ph, 0, n, 1, OP.max)
-        tt(dst, d0, "tB", o, pl, 0, n, 1, OP.max)
+    def double(lo, hi, n, th, dh, h0, dl, l0):
+        ph, pl, o = pair(lo, hi, n, th)
+        h0, l0 = (o if h0 is None else h0), (o if l0 is None else l0)
+        tt(dh, h0, "tH", o, ph, 0, n, 1, OP.max)
+        tt(dl, l0, "tB", o, pl, 0, n, 1, OP.max)
+        return o
 
     def gather(eng, dst, d0, src, a, b, off, c0, n, scale=1.0):
         ind = lambda: T[src][:, a:b].indirect(T[off][:, c0:c0 + n // 16])
@@ -170,14 +175,17 @@ def rank_program(g, core, T, topo):
     ts("eu", 0, "ei", 0, 128, 1)
 
     for a in range(0, 4096, 512):
-        for nm, m, c in (("f2", .5, 129 - .25), ("f4", .25, 129 - .375), ("f8", .125, 129 - .4375)):
-            if nm == "f8" and a < 1536:
-                act(nm, a, "raw", a, 512, AF.Copy, m, c)
-            else:
-                ts(nm, a, "raw", a, 512, .5, m, OP.mult, c, OP.add)
-        ps = newbank()
-        mm(ps, [("i1", "raw", a), ("i2", "f2", a), ("i8", "f4", a), ("i32", "f8", a)], 512)
-        act("win", a, ps, 0, 512, AF.Copy, 1.0, -129.0 * 42)
+        ts("f2", a, "raw", a, 512, .5, .5, OP.mult, 132 - .25, OP.add)
+        ts("f4", a, "raw", a, 512, .5, .25, OP.mult, 131 - .375, OP.add)
+        ps, terms = newbank(), [("i2", "f2", a), ("i8", "f4", a), ("i32", "f8", a)]
+        if a % 1024:
+            ts("f8", a, "raw", a, 512, .5, 8.0, OP.is_ge, -41.0, OP.add)
+            mm(ps, terms, 512)
+            tt("win", a, "raw", a, ps, 0, 512, 1, OP.add)
+        else:
+            act("f8", a, "raw", a, 512, AF.Copy, .125, 129 - .4375)
+            mm(ps, [("i1", "raw", a)] + terms, 512)
+            act("win", a, ps, 0, 512, AF.Copy, 1.0, -32.0 * (129 + 41))
 
     def zero(buf, a, b):
         G(lambda: g.iota(T[buf][:, a:b], [[0, b - a]], 0, 0, allow_small_or_imprecise_dtypes=True), b - a, [("i1", 0, 128)], [(buf, a, b)])
@@ -191,13 +199,13 @@ def rank_program(g, core, T, topo):
     for d in range(1, 5):
         base, nn, n = S[d] - 4096, S[d + 1] - S[d], CHUNK[d]
         for a in range(0, nn, n):
-            c = base + a
+            c, w, h = base + a, S[d] + a, n // 2
             gather("A", "ca", c, "win", S[d - 1], S[d], "lo", c // 16, n)
-            gather("V" if a == 0 else "A", "cb", c, "win", S[d - 1], S[d], "ro", c // 16, n)
+            gather("V" if a == 0 or d == 3 else "A", "cb", c, "win", S[d - 1], S[d], "ro", c // 16, n)
             if d < 3:
-                double(lambda e, c=c: [("ca", c + e), ("cb", c + e)], n // 2, "win", S[d] + a)
+                double([("ca", c), ("cb", c)], [("ca", c + h), ("cb", c + h)], h, "V", "win", w + h, "win", w)
             else:
-                single([("i1", "ca", c), ("i1", "cb", c)], n, "win", S[d] + a)
+                single([("i1", "ca", c), ("i1", "cb", c)], n, "win", w)
 
     for k, x, y in ((0, "cb", "lo"), (256, "ca", "ro")):
         ts("top", k, x, 3584, 256, .5, 85.0, OP.add)
@@ -212,19 +220,18 @@ def rank_program(g, core, T, topo):
     for a in (0, 2048):
         zero("outl", a, a + 2048)
         zero("outr", a, a + 2048)
-    for a in range(0, 2048, 512):
-        gather("A", "ine", a, "win", 0, S[5], "eu", a // 16, 512)
 
     for d in (3, 2, 1):
         base, nn = S[d] - 4096, S[d + 1] - S[d]
-        n = 256 if d == 3 else 512
+        n = 512 if d == 1 else 256
         lo_, hi_ = S[d - 1], S[d]
         for a in range(0, nn, n):
             c, w = base + a, S[d] + a
             if d < 3:
                 act("orb", c, "outr", w, n, AF.Copy, 4096.0)
-                for z in (0, 256):
-                    double(lambda e, c=c + z, w=w + z: [("outl", w + e), ("orb", c + e)], 128, "oo", c + z)
+                for z in range(0, n, 256):
+                    x, y = c + z, w + z
+                    double([("outl", y), ("orb", x)], [("outl", y + 128), ("orb", x + 128)], 128, "V", "oo", x + 128, "oo", x)
             V(lambda c=c, n=n, lo_=lo_, hi_=hi_: g.vector.tensor_tensor(
                 T.outl[:, lo_:hi_].indirect(T.lo[:, c // 16:(c + n) // 16]), T.oo[:, c:c + n], T.cb[:, c:c + n], OP.add), n, SC,
               [("oo", c, c + n), ("cb", c, c + n), ("lo", c // 16, (c + n) // 16)], [("outl", lo_, hi_)])
@@ -244,21 +251,32 @@ def rank_program(g, core, T, topo):
     for b in range(4):
         sel(32 * b, 128, "gsum", [[0, 8], [1, 4]], OP.is_equal, -b, 0)
 
-    for a in range(0, 2048, 512):
+    blocks, n, mid, mid2 = range(0, 2048, 512), 256, {}, {}
+    for a in blocks:
         gather("A", "ore", a, "outr", 0, S[5], "eu", a // 16, 512, scale=4096.0)
-        V(lambda a=a: g.vector.tensor_tensor(T.ole[:, a:a + 512], T.outl[:, 0:S[5]].indirect(T.eu[:, a // 16:a // 16 + 32]), T.ore[:, a:a + 512], OP.add), 512, GA,
-          [("outl", 0, S[5]), ("eu", a // 16, a // 16 + 32), ("ore", a, a + 512)], [("ole", a, a + 512)])
-    for a in range(0, 2048, 512):
-        n, h = 256, a + 256
-        ph, pl, o = pair([("ole", a)], [("ole", h)], n)
-        act("uh", o, ph, 0, n, AF.Relu)
-        act("ul", o, pl, 0, n, AF.Relu)
-        ph, pl, o2 = pair([("ine", a), ("tB", o), ("ul", o)], [("ine", h), ("tH", o), ("uh", o)], n)
-        act("uh", o2, ph, 0, n, AF.Relu)
+    for a in blocks:
+        gather("A", "ine", a, "win", 0, S[5], "eu", a // 16, 512)
+        ops[-1]["R"].append(("ore", 0, 1024))
+    for a in blocks:
+        if a >= 1024:
+            gather("A", "ole", a, "outl", 0, S[5], "eu", a // 16, 512)
+        else:
+            V(lambda a=a: g.vector.tensor_tensor(T.ole[:, a:a + 512], T.outl[:, 0:S[5]].indirect(T.eu[:, a // 16:a // 16 + 32]), T.ore[:, a:a + 512], OP.add), 512, GA,
+              [("outl", 0, S[5]), ("eu", a // 16, a // 16 + 32), ("ore", a, a + 512)], [("ole", a, a + 512)])
+    for a in blocks:
+        s = lambda x: [("ole", x)] + ([("ore", x)] if a >= 1024 else [])
+        mid[a] = double(s(a), s(a + n), n, "A", "uh", None, "ul", None)
+    for a in blocks:
+        h, o = a + n, mid[a]
+        ph, pl, o2 = pair([("ine", a), ("ul", o)], [("ine", h), ("uh", o)], n, None)
+        act("uh", o2, ph, 0, n, AF.Relu, 1.0, 128 * 256.0)
         act("ul", o2, pl, 0, n, AF.Relu)
+        mid2[a] = o2
+    for a in blocks:
+        h, o2 = a + n, mid2[a]
         pp, o = newbank(), newslot()
-        mm(pp, [("i1", "land", h), ("i1", "tH", o2), ("i1", "uh", o2), ("ip", "land", a), ("ip", "tB", o2), ("ip", "ul", o2)], n)
-        ts("tS", o, pp, 0, n, 1, 2.0 ** PB, OP.mult)
+        mm(pp, [("i1", "land", h), ("i1", "tY", o2), ("i1", "uh", o2), ("ip", "land", a), ("ip", "tB", o2), ("ip", "ul", o2)], n)
+        ts("tS", o, pp, 0, n, 1, 2.0 ** PB, OP.mult, float(-128 << PB), OP.add)
         for m, z in ((0xAA << PB, h), (0xAA, a)):
             o2 = newslot()
             ts("tT", o2, "tS", o, n, 1, m, OP.bitwise_and)
@@ -277,8 +295,7 @@ def rank_program(g, core, T, topo):
             V(lambda ps=ps, kk=kk, k=k, c=c: g.vector.tensor_scalar(T.key[:, c:c + 64], T[ps][0:32, 64 * kk:64 * kk + 64], float(k), None, OP.add),
               64, 1, [(ps, 0, 512)], [("key", c, c + 64)])
             if k:
-                tt("key", r0 + 64, "key", 0 if k == 1 else r0, "key", c, 64, 2, OP.min)
-    ts("keyi", 0, "key", 960, 64, 1)
+                tt("key" if k < 7 else "keyi", r0 + 64 if k < 7 else 0, "key", 0 if k == 1 else r0, "key", c, 64, 2, OP.min)
     ts("keyi", 64, "keyi", 0, 64, 1, 3, OP.logical_shift_right)
     ts("keyi", 128, "keyi", 0, 64, 1, 7, OP.bitwise_and)
     ts("res", 0, "keyi", 64, 64, 1)
@@ -327,7 +344,7 @@ def run(g, T, ops):
         e = ops[best]["eng"]
         bt = max(est[best], free.get(e, 0.0) if e else 0.0)
         if e:
-            cand = [i for i in ready if ops[i]["eng"] == e and max(est[i], free.get(e, 0.0)) <= bt + 300]
+            cand = [i for i in ready if ops[i]["eng"] == e and max(est[i], free.get(e, 0.0)) <= bt + 60]
             best = max(cand, key=lambda i: (tail[i], -i))
             bt = max(est[best], free.get(e, 0.0))
             free[e] = bt + ops[best]["cost"]

@@ -4,18 +4,23 @@ from concourse.mybir import AluOpType as OP, ActivationFunctionType as AF
 S = [0, 4096, 6144, 7168, 7680, 7936]
 NT = 12
 PB = 14
-CHUNK = {1: 512, 2: 256, 3: 256, 4: 128}
+CHUNK = {1: 512, 2: 256, 3: 256, 4: 256}
 GA, SC = 1.56, 3.8
+LATE = 12000
+BY_A = ((1, 0), (1, 1024))
+BY_V = (0, 1536)
+BY_MAX = (512, 1536)
 
 BUFS = {
-    "bfloat16": {"raw": 4096, "f2": 4096, "f4": 4096, "f8": 4096, "win": 7936, "outl": 7936, "ca": 3840, "cb": 3840, "top": 512,
-                 "orb": 3072, "oo": 3584, "tY": 256 * NT, "tB": 256 * NT, "tH": 256 * NT, "uh": 256 * NT, "ul": 256 * NT,
-                 "ole": 2048, "ore": 2048, "ine": 2048, "zz": 2048, "land": 2048, "clout": 2048, "one": 128, "gsum": 192},
-    "float32": {"outr": 7936, "pre": 2048, "key": 64 * 17, "res": 128},
-    "int32": {"tS": 256 * NT, "tT": 256 * NT, "li": 240, "ri": 240, "ci": 128, "ei": 128, "keyi": 192},
-    "uint16": {"lo": 240, "ro": 240, "cu": 128, "cin": 128, "eu": 128},
+    "bfloat16": {"raw": 4096, "f2": 2048, "f4": 2048, "f8": 2048, "win": 7936, "X": 5888, "Y": 4112, "ca": 1792, "cb": 1792,
+                 "top": 512, "oo": 1536, "tY": 256 * NT, "tB": 256 * NT, "uh": 256 * NT, "ul": 256 * NT,
+                 "ole": 2048, "ye": 2048, "ine": 2048, "zz": 2048, "land": 2048, "clout": 2048, "one": 256, "gsum": 192,
+                 "ku": 128, "kc": 128, "kd": 128, "ke": 128, "kmat": 256, "inv": 64},
+    "float32": {"key": 512, "res": 128, "W": 7936, "val": 4096, "onef": 128, "i1f": 128, "selm": 2048},
+    "int32": {"tS": 256 * NT, "tT": 256 * NT, "li": 240, "ri": 240, "ci": 128, "ei": 128, "keyi": 192, "ej": 128, "ek": 128, "el": 128},
+    "uint16": {"lo": 240, "ro": 240, "cu": 128, "cin": 128, "eu": 128, "e1": 128, "e2": 128},
 }
-DIAG = {"i1": 1.0, "i2": 2.0, "i8": 8.0, "i32": 32.0, "ik": -256.0, "im": 2.0 ** -12, "ip": 2.0 ** -PB, "iq": 2.0 ** PB}
+DIAG = {"i1": 1.0, "i2": 2.0, "i8": 8.0, "i32": 32.0, "ik": -256.0, "ip": 2.0 ** -PB, "iq": 2.0 ** PB}
 SCRATCH = {}
 for _t in BUFS:
     for _b in BUFS[_t]:
@@ -88,48 +93,67 @@ def rank_program(g, core, T, topo):
         A(lambda: g.scalar.activation(T[dst][:, d0:d0 + n], T[src][:, s0:s0 + n], func, bias=bias, scale=scale), n, 1,
           [reg(src, s0, n)], [reg(dst, d0, n)])
 
-    def single(terms, n, dst, d0):
-        ps, pw, o = newbank(), newbank(), newslot()
-        mm(ps, terms, n)
-        mm(pw, terms, n, stop=False)
-        ts("tS", o, ps, 0, n, 1)
-        ts("tT", o, "tS", o, n, 1, 1, OP.logical_shift_right, 0x55, OP.bitwise_and)
-        ts("tB", o, "tT", o, n, 1)
-        mm(pw, [("ik", "tB", o)], n, start=False)
-        tt(dst, d0, "tB", o, pw, 0, n, 1, OP.max)
+    def fill(buf, p0, p1, a, b, x):
+        V(lambda: g.vector.memset(T[buf][p0:p1, a:b], x), b - a, .5, [], [(buf, a, b)])
 
-    def pair(lo, hi, n, th):
-        pp, ph, pl, o = newbank(), newbank(), newbank(), newslot()
+    def split(lo, hi, n, kind):
+        pp, o = newbank(), newslot()
+        m = 0x55 if kind == "out" else 0xD5
         mm(pp, [("i1", b, a) for b, a in hi] + [("ip", b, a) for b, a in lo], n)
-        mm(ph, [("i1", b, a) for b, a in hi], n, stop=False)
-        mm(pl, [("i1", b, a) for b, a in lo], n, stop=False)
-        ts("tS", o, pp, 0, n, 1, 2.0 ** PB, OP.mult, float(2 ** (PB + 8)), OP.add)
-        ts("tT", o, "tS", o, n, 1, 1, OP.logical_shift_right, 0x55 + (0x55 << PB) + (1 << PB + 7), OP.bitwise_and)
-        ts("tY", o, "tT", o, n, 1, 2.0 ** -PB, OP.mult)
-        mm(pp, [("iq", "tY", o)], n)
+        if kind == "edge":
+            ts("tS", o, pp, 0, n, 1, 2.0 ** PB, OP.mult, float((256 << PB) + 256), OP.add)
+        else:
+            ts("tS", o, pp, 0, n, 1, 2.0 ** PB, OP.mult)
+        ts("tT", o, "tS", o, n, 1, 1, OP.logical_shift_right, m + (m << PB), OP.bitwise_and)
+        if kind == "out":
+            ts("tY", o, "tT", o, n, 1, 2.0 ** -PB, OP.mult, -128.0, OP.add)
+        else:
+            ts("tY", o, "tT", o, n, 1, 2.0 ** -PB, OP.mult)
+        mm(pp, [("iq", "tY", o)] + ([("kc", "one", 0)] if kind == "out" else []), n)
         tt("tB", o, "tT", o, pp, 0, n, 1, OP.subtract)
-        if th == "A":
-            act("tH", o, "tY", o, n, AF.Copy, 1.0, -128.0)
-        elif th == "V":
-            ts("tH", o, "tY", o, n, .5, -128.0, OP.add)
-        mm(ph, [("ik", "tH" if th else "tY", o)], n, start=False)
+        return o
+
+    def pair(lo, hi, n, kind, const=None):
+        ph, pl = newbank(), newbank()
+        k = [(const, "one", 0)] if const else []
+        o = split(lo, hi, n, kind)
+        mm(ph, [("i1", b, a) for b, a in hi] + k, n, stop=False)
+        mm(pl, [("i1", b, a) for b, a in lo] + k, n, stop=False)
+        mm(ph, [("ik", "tY", o)], n, start=False)
         mm(pl, [("ik", "tB", o)], n, start=False)
         return ph, pl, o
 
-    def double(lo, hi, n, th, dh, h0, dl, l0):
-        ph, pl, o = pair(lo, hi, n, th)
+    def double(lo, hi, n, kind, dh, h0, dl, l0):
+        ph, pl, o = pair(lo, hi, n, kind, {"out": "kd", "in": "ku", "edge": "ke"}[kind])
         h0, l0 = (o if h0 is None else h0), (o if l0 is None else l0)
-        tt(dh, h0, "tH", o, ph, 0, n, 1, OP.max)
+        tt(dh, h0, "tY", o, ph, 0, n, 1, OP.max)
         tt(dl, l0, "tB", o, pl, 0, n, 1, OP.max)
         return o
 
-    def gather(eng, dst, d0, src, a, b, off, c0, n, scale=1.0):
+    def double_a(lo, hi, n, dh, h0, dl, l0):
+        ph, pl, o = pair(lo, hi, n, "out")
+        for u, ps, t, dst, d0 in (("uh", ph, "tY", dh, h0), ("ul", pl, "tB", dl, l0)):
+            act(u, o, ps, 0, n, AF.Relu, 1.0, -128 * 256.0)
+            pf = newbank()
+            mm(pf, [("i1", t, o), ("i1", u, o)], n)
+            act(dst, d0, pf, 0, n)
+
+    def gather(eng, dst, d0, src, a, b, off, c0, n):
         ind = lambda: T[src][:, a:b].indirect(T[off][:, c0:c0 + n // 16])
         R, W = [(src, a, b), (off, c0, c0 + n // 16)], [(dst, d0, d0 + n)]
         if eng == "V":
             V(lambda: g.vector.tensor_copy(T[dst][:, d0:d0 + n], ind()), n, GA, R, W)
         else:
-            A(lambda: g.scalar.activation(T[dst][:, d0:d0 + n], ind(), AF.Copy, scale=scale), n, GA, R, W)
+            A(lambda: g.scalar.activation(T[dst][:, d0:d0 + n], ind(), AF.Copy), n, GA, R, W)
+
+    def silu(win, a, b, off, c0, src, s0, n):
+        A(lambda: g.scalar.activation(T[win][:, a:b].indirect(T[off][:, c0:c0 + n // 16]), T[src][:, s0:s0 + n], AF.Silu), n, SC,
+          [(src, s0, s0 + n), (off, c0, c0 + n // 16)], [(win, a, b)])
+        ops[-1]["late"] = LATE
+
+    CA = lambda c: ("Y", 2048 + c) if c < 2048 else ("ca", c - 2048)
+    CB = lambda c: ("Y", c) if c < 2048 else ("cb", c - 2048)
+    OO = lambda c: ("X", c) if c < 2048 else ("oo", c - 2048)
 
     def load(eng, i, dst, a, b, src, lat):
         q = g.sync if eng == "Y" else g.scalar
@@ -142,11 +166,20 @@ def rank_program(g, core, T, topo):
     load("A", 6, "ri", 0, 240, "right", 3000)
     load("Y", 7, "ei", 0, 128, "edge", 6500)
 
-    V(lambda: g.vector.memset(T.one[:], 1.0), 128, .5, [], [("one", 0, 128)])
-    G(lambda: g.affine_select(T.i1[:], T.one[:], [[-1, 128]], OP.is_equal, 0.0, 0, 1), 128, [("one", 0, 128)], [("i1", 0, 128)])
+    fill("one", 0, 128, 0, 256, 1.0)
+    G(lambda: g.affine_select(T.i1[:], T.one[:, 0:128], [[-1, 128]], OP.is_equal, 0.0, 0, 1), 128, [("one", 0, 128)], [("i1", 0, 128)])
     for nm in DIAG:
         if nm != "i1":
             ts(nm, 0, "i1", 0, 128, .5, DIAG[nm], OP.mult)
+    fill("ku", 0, 128, 0, 128, 255.0)
+    fill("kc", 0, 64, 0, 128, 2.0 ** (PB + 1))
+    fill("kc", 64, 128, 0, 128, 2.0)
+    fill("kd", 0, 64, 0, 128, -512.0)
+    fill("kd", 64, 128, 0, 128, -2.0)
+    fill("ke", 0, 64, 0, 128, 512.0)
+    fill("ke", 64, 128, 0, 128, 2.0)
+    fill("onef", 0, 128, 0, 128, 1.0)
+    fill("inv", 0, 128, 0, 64, 2.0 ** -7)
 
     ts("cu", 0, "ci", 0, 128, 1)
     for d in range(1, 5):
@@ -175,72 +208,84 @@ def rank_program(g, core, T, topo):
     ts("eu", 0, "ei", 0, 128, 1)
 
     for a in range(0, 4096, 512):
-        ts("f2", a, "raw", a, 512, .5, .5, OP.mult, 132 - .25, OP.add)
-        ts("f4", a, "raw", a, 512, .5, .25, OP.mult, 131 - .375, OP.add)
-        ps, terms = newbank(), [("i2", "f2", a), ("i8", "f4", a), ("i32", "f8", a)]
+        f = a % 2048
+        ts("f2", f, "raw", a, 512, .5, .5, OP.mult, 132 - .25, OP.add)
+        ts("f4", f, "raw", a, 512, .5, .25, OP.mult, 131 - .375, OP.add)
+        ps, terms = newbank(), [("i2", "f2", f), ("i8", "f4", f), ("i32", "f8", f)]
         if a % 1024:
-            ts("f8", a, "raw", a, 512, .5, 8.0, OP.is_ge, -41.0, OP.add)
+            ts("f8", f, "raw", a, 512, .5, 8.0, OP.is_ge, -37.0, OP.add)
             mm(ps, terms, 512)
             tt("win", a, "raw", a, ps, 0, 512, 1, OP.add)
         else:
-            act("f8", a, "raw", a, 512, AF.Copy, .125, 129 - .4375)
+            act("f8", f, "raw", a, 512, AF.Copy, .125, 129 - .4375)
             mm(ps, [("i1", "raw", a)] + terms, 512)
-            act("win", a, ps, 0, 512, AF.Copy, 1.0, -32.0 * (129 + 41))
+            act("win", a, ps, 0, 512, AF.Copy, 1.0, 128.0 - 32.0 * (129 + 41))
 
-    def zero(buf, a, b):
-        G(lambda: g.iota(T[buf][:, a:b], [[0, b - a]], 0, 0, allow_small_or_imprecise_dtypes=True), b - a, [("i1", 0, 128)], [(buf, a, b)])
+    def ramp(buf, a, n, step, base):
+        G(lambda: g.iota(T[buf][:, a:a + n], [[step, n]], base, 0, allow_small_or_imprecise_dtypes=True), n, [("i1", 0, 128)], [(buf, a, a + n)])
 
-    V(lambda: g.vector.memset(T.outl[:, S[4]:S[5]], 85.0), 256, .5, [], [("outl", S[4], S[5])])
-    for d in (2, 1):
-        zero("outl", S[d], S[d + 1])
-        zero("outr", S[d], S[d + 1])
-    zero("outr", S[3], S[5])
+    V(lambda: g.vector.memset(T.X[:, S[4] - 2048:S[5] - 2048], 85.0), 256, .5, [], [("X", S[4] - 2048, S[5] - 2048)])
+    for a in range(0, 4096, 512):
+        ramp("val", a, 512, 1, 4096 + a)
+    ramp("Y", 4096, 16, 0, 0)
+    for a in range(4096, S[5], 1280):
+        ramp("W", a, 1280, 1, 4096 + a)
+    G(lambda: g.affine_select(T.i1f[:], T.onef[:], [[-1, 128]], OP.is_equal, 0.0, 0, 1), 128, [("onef", 0, 128)], [("i1f", 0, 128)])
+    for s in range(16):
+        G(lambda s=s: g.affine_select(T.selm[:, 128 * s:128 * s + 128], T.i1f[:], [[0, 8], [1, 16]], OP.is_equal, 0.0, -s, 0), 128,
+          [("i1f", 0, 128)], [("selm", 128 * s, 128 * s + 128)])
+    G(lambda: g.iota(T.kmat[:], [[1, 8], [0, 32]], 0, 0, allow_small_or_imprecise_dtypes=True), 256, [], [("kmat", 0, 256)])
+
+    for a in range(0, 2048, 256):
+        silu("W", 0, 4096, "lo", a // 16, "val", a, 256)
+        silu("W", 0, 4096, "ro", a // 16, "val", 2048 + a, 256)
 
     for d in range(1, 5):
         base, nn, n = S[d] - 4096, S[d + 1] - S[d], CHUNK[d]
         for a in range(0, nn, n):
             c, w, h = base + a, S[d] + a, n // 2
-            gather("A", "ca", c, "win", S[d - 1], S[d], "lo", c // 16, n)
-            gather("V" if a == 0 or d == 3 else "A", "cb", c, "win", S[d - 1], S[d], "ro", c // 16, n)
-            if d < 3:
-                double([("ca", c), ("cb", c)], [("ca", c + h), ("cb", c + h)], h, "V", "win", w + h, "win", w)
-            else:
-                single([("i1", "ca", c), ("i1", "cb", c)], n, "win", w)
+            gather("A", *CA(c), "win", S[d - 1], S[d], "lo", c // 16, n)
+            gather("V" if a % 1024 == 0 or d == 3 else "A", *CB(c), "win", S[d - 1], S[d], "ro", c // 16, n)
+            double([CA(c), CB(c)], [CA(c + h), CB(c + h)], h, "in", "win", w + h, "win", w)
 
     for k, x, y in ((0, "cb", "lo"), (256, "ca", "ro")):
-        ts("top", k, x, 3584, 256, .5, 85.0, OP.add)
-        V(lambda k=k, y=y: g.vector.tensor_copy(T.outl[:, S[3]:S[4]].indirect(T[y][:, 224:240]), T.top[:, k:k + 256]), 256, SC,
-          [("top", k, k + 256), (y, 224, 240)], [("outl", S[3], S[4])])
-    ts("oo", 3072, "outl", S[3], 512, .5, -85.0, OP.add)
+        ts("top", k, x, 1536, 256, .5, 85.0 - 128.0, OP.add)
+        V(lambda k=k, y=y: g.vector.tensor_copy(T.X[:, S[3] - 2048:S[4] - 2048].indirect(T[y][:, 224:240]), T.top[:, k:k + 256]), 256, SC,
+          [("top", k, k + 256), (y, 224, 240)], [("X", S[3] - 2048, S[4] - 2048)])
+    ts("oo", 1024, "X", S[3] - 2048, 512, .5, -85.0 - 128.0, OP.add)
 
     for q in others + [rank]:
         dst, off = ("land", "cu") if q == rank else ("clout", "cin")
         gather("A", dst, 512 * q, "win", 0, S[5], off, 32 * q, 512)
     exchange("clout", "land", 512, "clr", 35000)
-    for a in (0, 2048):
-        zero("outl", a, a + 2048)
-        zero("outr", a, a + 2048)
+
+    for a in range(0, 2048, 512):
+        gather("A", "val", a, "W", 0, S[5], "eu", a // 16, 512)
+    ps = newbank()
+    for s in range(16):
+        P([lambda s=s, ps=ps: g.tensor.matmul(T[ps][:, 0:128], T.selm[:, 128 * s:128 * s + 128], T.val[:, s:2048:16], s == 0, s == 15)],
+          512, [("selm", 128 * s, 128 * s + 128), ("val", 0, 2048)], [(ps, 0, 512)])
+    ts("ej", 0, ps, 0, 128, 1, -4095.75, OP.add)
+    ts("ek", 0, "ej", 0, 128, 1, 2048.0, OP.is_ge, -2048.0, OP.mult)
+    tt("el", 0, "ej", 0, "ek", 0, 128, 2, OP.add)
+    ts("e2", 0, "ej", 0, 128, 1, 4096.0, OP.min)
+    ts("e1", 0, "el", 0, 128, 1)
 
     for d in (3, 2, 1):
-        base, nn = S[d] - 4096, S[d + 1] - S[d]
-        n = 512 if d == 1 else 256
-        lo_, hi_ = S[d - 1], S[d]
+        base, nn, n, h = S[d] - 4096, S[d + 1] - S[d], 512, 256
+        lo_, hi_ = S[d - 1] - 2048, S[d] - 2048
         for a in range(0, nn, n):
-            c, w = base + a, S[d] + a
-            if d < 3:
-                act("orb", c, "outr", w, n, AF.Copy, 4096.0)
-                for z in range(0, n, 256):
-                    x, y = c + z, w + z
-                    double([("outl", y), ("orb", x)], [("outl", y + 128), ("orb", x + 128)], 128, "V", "oo", x + 128, "oo", x)
-            V(lambda c=c, n=n, lo_=lo_, hi_=hi_: g.vector.tensor_tensor(
-                T.outl[:, lo_:hi_].indirect(T.lo[:, c // 16:(c + n) // 16]), T.oo[:, c:c + n], T.cb[:, c:c + n], OP.add), n, SC,
-              [("oo", c, c + n), ("cb", c, c + n), ("lo", c // 16, (c + n) // 16)], [("outl", lo_, hi_)])
-            ps, p = newbank(), c % 2048
-            mm(ps, [("im", "oo", c), ("im", "ca", c)], n)
-            act("pre", p, ps, 0, n)
-            A(lambda p=p, c=c, n=n, lo_=lo_, hi_=hi_: g.scalar.activation(
-                T.outr[:, lo_:hi_].indirect(T.ro[:, c // 16:(c + n) // 16]), T.pre[:, p:p + n], AF.Tanh), n, SC,
-              [("pre", p, p + n), ("ro", c // 16, (c + n) // 16)], [("outr", lo_, hi_)])
+            c, w = base + a, S[d] + a - 2048
+            if (d, a) in BY_A:
+                double_a([("X", w)], [("X", w + h)], h, *OO(c + h), *OO(c))
+            elif d < 3:
+                double([("X", w)], [("X", w + h)], h, "out", *OO(c + h), *OO(c))
+            if d > 1:
+                q = c - 2048
+                for off, sib in (("lo", "cb"), ("ro", "ca")):
+                    V(lambda off=off, sib=sib, c=c, q=q, n=n, lo_=lo_, hi_=hi_: g.vector.tensor_tensor(
+                        T.X[:, lo_:hi_].indirect(T[off][:, c // 16:(c + n) // 16]), T.oo[:, q:q + n], T[sib][:, q:q + n], OP.add), n, SC,
+                      [("oo", q, q + n), (sib, q, q + n), (off, c // 16, (c + n) // 16)], [("X", lo_, hi_)])
 
     def sel(d0, s0, src, pat, o, base, cm):
         G(lambda: g.affine_select(T.gsum[:, d0:d0 + 32], T[src][:, s0:s0 + 32], pat, o, 0.0, base, cm), 32, [reg(src, s0, 32)], [("gsum", d0, d0 + 32)])
@@ -253,55 +298,60 @@ def rank_program(g, core, T, topo):
 
     blocks, n, mid, mid2 = range(0, 2048, 512), 256, {}, {}
     for a in blocks:
-        gather("A", "ore", a, "outr", 0, S[5], "eu", a // 16, 512, scale=4096.0)
-    for a in blocks:
         gather("A", "ine", a, "win", 0, S[5], "eu", a // 16, 512)
-        ops[-1]["R"].append(("ore", 0, 1024))
     for a in blocks:
-        if a >= 1024:
-            gather("A", "ole", a, "outl", 0, S[5], "eu", a // 16, 512)
+        gather("A", "ye", a, "Y", 0, 4112, "e2", a // 16, 512)
+    for a in blocks:
+        if a in BY_V:
+            V(lambda a=a: g.vector.tensor_tensor(T.ole[:, a:a + 512], T.X[:, 0:S[5] - 2048].indirect(T.e1[:, a // 16:a // 16 + 32]), T.ye[:, a:a + 512], OP.add), 512, GA,
+              [("X", 0, S[5] - 2048), ("e1", a // 16, a // 16 + 32), ("ye", a, a + 512)], [("ole", a, a + 512)])
         else:
-            V(lambda a=a: g.vector.tensor_tensor(T.ole[:, a:a + 512], T.outl[:, 0:S[5]].indirect(T.eu[:, a // 16:a // 16 + 32]), T.ore[:, a:a + 512], OP.add), 512, GA,
-              [("outl", 0, S[5]), ("eu", a // 16, a // 16 + 32), ("ore", a, a + 512)], [("ole", a, a + 512)])
+            gather("A", "ole", a, "X", 0, S[5] - 2048, "e1", a // 16, 512)
     for a in blocks:
-        s = lambda x: [("ole", x)] + ([("ore", x)] if a >= 1024 else [])
-        mid[a] = double(s(a), s(a + n), n, "A", "uh", None, "ul", None)
+        sum_ = lambda x: [("ole", x)] + ([] if a in BY_V else [("ye", x)])
+        if a in BY_MAX:
+            o = double(sum_(a), sum_(a + n), n, "edge", "uh", None, "ul", None)
+        else:
+            ph, pl, o = pair(sum_(a), sum_(a + n), n, "edge")
+            act("uh", o, ph, 0, n, AF.Relu, 1.0, 128 * 256.0)
+            act("ul", o, pl, 0, n, AF.Relu, 1.0, 128 * 256.0)
+        mid[a] = o
     for a in blocks:
         h, o = a + n, mid[a]
-        ph, pl, o2 = pair([("ine", a), ("ul", o)], [("ine", h), ("uh", o)], n, None)
-        act("uh", o2, ph, 0, n, AF.Relu, 1.0, 128 * 256.0)
-        act("ul", o2, pl, 0, n, AF.Relu)
+        tl, th = ([], []) if a in BY_MAX else ([("tB", o)], [("tY", o)])
+        ph, pl, o2 = pair([("ine", a), ("ul", o)] + tl, [("ine", h), ("uh", o)] + th, n, "in")
+        act("uh", o2, ph, 0, n, AF.Relu, 1.0, 127 * 256.0)
+        act("ul", o2, pl, 0, n, AF.Relu, 1.0, 127 * 256.0)
         mid2[a] = o2
     for a in blocks:
         h, o2 = a + n, mid2[a]
-        pp, o = newbank(), newslot()
-        mm(pp, [("i1", "land", h), ("i1", "tY", o2), ("i1", "uh", o2), ("ip", "land", a), ("ip", "tB", o2), ("ip", "ul", o2)], n)
-        ts("tS", o, pp, 0, n, 1, 2.0 ** PB, OP.mult, float(-128 << PB), OP.add)
-        for m, z in ((0xAA << PB, h), (0xAA, a)):
-            o2 = newslot()
-            ts("tT", o2, "tS", o, n, 1, m, OP.bitwise_and)
-            ts("zz", z, "tT", o2, n, 1, 0.0, OP.is_equal)
+        o = split([("land", a), ("tB", o2), ("ul", o2)], [("land", h), ("tY", o2), ("uh", o2)], n, "in")
+        act("zz", h, "tY", o, n, AF.Relu, -1.0, 129.0)
+        act("zz", a, "tB", o, n, AF.Relu, -1.0, 129.0)
         ps = newbank()
         fns = []
         for kk in range(2):
+            k = a // 256 + kk
             for b in range(4):
                 fns.append(lambda kk=kk, b=b, ps=ps, a=a: g.tensor.matmul(
                     T[ps][0:32, 64 * kk:64 * kk + 64], T.gsum[:, 32 * b:32 * b + 32],
-                    T.zz[:, a + 256 * kk + 64 * b:a + 256 * kk + 64 * b + 64], b == 0, b == 3))
-        P(fns, 64, [("gsum", 0, 128), ("zz", a, a + 512)], [(ps, 0, 512)])
-        for kk in range(2):
-            k = a // 256 + kk
-            c, r0 = 64 * k, 64 * (7 + k)
-            V(lambda ps=ps, kk=kk, k=k, c=c: g.vector.tensor_scalar(T.key[:, c:c + 64], T[ps][0:32, 64 * kk:64 * kk + 64], float(k), None, OP.add),
-              64, 1, [(ps, 0, 512)], [("key", c, c + 64)])
-            if k:
-                tt("key" if k < 7 else "keyi", r0 + 64 if k < 7 else 0, "key", 0 if k == 1 else r0, "key", c, 64, 2, OP.min)
+                    T.zz[:, a + 256 * kk + 64 * b:a + 256 * kk + 64 * b + 64], b == 0, False))
+            fns.append(lambda kk=kk, k=k, ps=ps: g.tensor.matmul(
+                T[ps][0:32, 64 * kk:64 * kk + 64], T.kmat[:, 32 * k:32 * k + 32], T.inv[:], False, True))
+        P(fns, 64, [("gsum", 0, 128), ("zz", a, a + 512), ("kmat", 0, 256), ("inv", 0, 64)], [(ps, 0, 512)])
+        r = a // 4
+        if a == 0:
+            V(lambda ps=ps: g.vector.tensor_copy(T.key[:, 0:128], T[ps][0:32, 0:128]), 128, 1, [(ps, 0, 512)], [("key", 0, 128)])
+        else:
+            V(lambda ps=ps, r=r: g.vector.tensor_tensor(T.key[:, r:r + 128], T.key[:, r - 128:r], T[ps][0:32, 0:128], OP.min), 128, 1,
+              [(ps, 0, 512), ("key", r - 128, r)], [("key", r, r + 128)])
+    tt("keyi", 0, "key", 384, "key", 448, 64, 2, OP.min)
     ts("keyi", 64, "keyi", 0, 64, 1, 3, OP.logical_shift_right)
     ts("keyi", 128, "keyi", 0, 64, 1, 7, OP.bitwise_and)
     ts("res", 0, "keyi", 64, 64, 1)
     ts("res", 64, "keyi", 128, 64, 1)
     op("Y", [lambda: g.sync.dma_start(T.cost[:], T.res[:, 0:64])], 120, [("res", 0, 64)], [], lat=2000, dma="ld8", inc=16)
-    op("Y", [lambda: g.sync.dma_start(T["first"][:], T.res[:, 64:128])], 120, [("res", 64, 128)], [], lat=2000, dma="ld9", inc=16)
+    op("A", [lambda: g.scalar.dma_start(T["first"][:], T.res[:, 64:128])], 120, [("res", 64, 128)], [], lat=2000, dma="ld9", inc=16)
 
     run(g, T, ops)
 
@@ -334,6 +384,8 @@ def run(g, T, ops):
     tail = [0.0] * n
     for i in range(n - 1, -1, -1):
         tail[i] = ops[i]["cost"] + ops[i]["lat"] + max([tail[k] + 80 for k in succ[i]] or [0.0])
+    for i in range(n):
+        tail[i] -= ops[i].get("late", 0)
     free, fin = {}, [0.0] * n
     need = [len(d) for d in deps]
     ready = [i for i in range(n) if not need[i]]

@@ -7,17 +7,20 @@ PB = 14
 CHUNK = {1: 512, 2: 256, 3: 256, 4: 256}
 GA, SC = 1.56, 3.8
 LATE = 12000
-BY_A = ((1, 0), (1, 1024))
-BY_V = (0, 1536)
-BY_MAX = (512, 1536)
+BY_A = ((1, 0),)
+BY_V = (0, 1024)
+BY_MAX = (1024, 1536)
+BY_REL = (0,)
+CONV_A = (512, 1024, 1536, 3072)
+ON_V = (("r", 0), ("r", 1024), ("r", 2048), ("r", 3072), ("r", 3328), ("r", 3584))
 
 BUFS = {
     "bfloat16": {"raw": 4096, "f2": 2048, "f4": 2048, "f8": 2048, "win": 7936, "X": 5888, "Y": 4112, "ca": 1792, "cb": 1792,
-                 "top": 512, "oo": 1536, "tY": 256 * NT, "tB": 256 * NT, "uh": 256 * NT, "ul": 256 * NT,
-                 "ole": 2048, "ye": 2048, "ine": 2048, "zz": 2048, "land": 2048, "clout": 2048, "one": 256, "gsum": 192,
+                 "oo": 1024, "tY": 256 * NT, "tB": 256 * NT, "uh": 256 * NT, "ul": 256 * NT,
+                 "ole": 2048, "ye": 2048, "ine": 2048, "zz": 2048, "land": 2048, "clout": 2048, "one": 512, "gsum": 192,
                  "ku": 128, "kc": 128, "kd": 128, "ke": 128, "kmat": 256, "inv": 64},
-    "float32": {"key": 512, "res": 128, "W": 7936, "val": 4096, "onef": 128, "i1f": 128, "selm": 2048},
-    "int32": {"tS": 256 * NT, "tT": 256 * NT, "li": 240, "ri": 240, "ci": 128, "ei": 128, "keyi": 192, "ej": 128, "ek": 128, "el": 128},
+    "float32": {"key": 512, "res": 128, "W": 7936, "val": 4096, "ek": 128, "el": 128, "onef": 128, "i1f": 128, "selm": 2048},
+    "int32": {"tS": 256 * NT, "tT": 256 * NT, "li": 240, "ri": 240, "ci": 128, "ei": 128, "keyi": 192},
     "uint16": {"lo": 240, "ro": 240, "cu": 128, "cin": 128, "eu": 128, "e1": 128, "e2": 128},
 }
 DIAG = {"i1": 1.0, "i2": 2.0, "i8": 8.0, "i32": 32.0, "ik": -256.0, "ip": 2.0 ** -PB, "iq": 2.0 ** PB}
@@ -50,20 +53,22 @@ def rank_program(g, core, T, topo):
         op("A", [fn], 50 + 1.04 * n * c, R, W)
 
     def P(fns, n, R, W):
-        op("P", fns, 40 + 0.5 * max(64, n) * len(fns), R, W)
+        op("P", fns, 20 + 0.45 * max(64, n) * len(fns), R, W)
 
     def G(fn, n, R, W):
         op("G", [fn], 150 + 2.08 * n, R, W)
 
+    on = lambda k, a: "V" if (k, a) in ON_V else "A"
     bank, slots = [0], [0]
 
     def newbank():
         bank[0] += 1
         return "ps%d" % ((bank[0] - 1) % 8)
 
-    def newslot():
-        slots[0] += 1
-        return 256 * ((slots[0] - 1) % NT)
+    def newslot(n):
+        a = slots[0] if slots[0] % (256 * NT) + n <= 256 * NT else slots[0] + 256
+        slots[0] = a + n
+        return a % (256 * NT)
 
     def reg(b, a, n):
         return (b, 0, 512) if b[:2] == "ps" else (b, a, a + n)
@@ -96,55 +101,57 @@ def rank_program(g, core, T, topo):
     def fill(buf, p0, p1, a, b, x):
         V(lambda: g.vector.memset(T[buf][p0:p1, a:b], x), b - a, .5, [], [(buf, a, b)])
 
-    def split(lo, hi, n, kind):
-        pp, o = newbank(), newslot()
-        m = 0x55 if kind == "out" else 0xD5
+    def split(lo, hi, n, kind, z=None):
+        pp, o = newbank(), newslot(max(n, 256))
         mm(pp, [("i1", b, a) for b, a in hi] + [("ip", b, a) for b, a in lo], n)
-        if kind == "edge":
+        if kind in ("edge", "out"):
             ts("tS", o, pp, 0, n, 1, 2.0 ** PB, OP.mult, float((256 << PB) + 256), OP.add)
         else:
             ts("tS", o, pp, 0, n, 1, 2.0 ** PB, OP.mult)
-        ts("tT", o, "tS", o, n, 1, 1, OP.logical_shift_right, m + (m << PB), OP.bitwise_and)
-        if kind == "out":
-            ts("tY", o, "tT", o, n, 1, 2.0 ** -PB, OP.mult, -128.0, OP.add)
-        else:
-            ts("tY", o, "tT", o, n, 1, 2.0 ** -PB, OP.mult)
+        ts("tT", o, "tS", o, n, 1, 1, OP.logical_shift_right, (0x55 if kind == "test" else 0xD5) + (0xD5 << PB), OP.bitwise_and)
+        ts("tY", o, "tT", o, n, 1, 2.0 ** -PB, OP.mult, *((-256.0, OP.add) if kind == "out" else ()))
         mm(pp, [("iq", "tY", o)] + ([("kc", "one", 0)] if kind == "out" else []), n)
-        tt("tB", o, "tT", o, pp, 0, n, 1, OP.subtract)
+        if kind == "test":
+            tt("zz", z, "tT", o, pp, 0, n, 1, OP.is_equal)
+        else:
+            tt("tB", o, "tT", o, pp, 0, n, 1, OP.subtract)
         return o
 
-    def pair(lo, hi, n, kind, const=None):
-        ph, pl = newbank(), newbank()
-        k = [(const, "one", 0)] if const else []
-        o = split(lo, hi, n, kind)
-        mm(ph, [("i1", b, a) for b, a in hi] + k, n, stop=False)
-        mm(pl, [("i1", b, a) for b, a in lo] + k, n, stop=False)
+    def pair(lo, hi, n, kind, const, his, los):
+        o, ph = split(lo, hi, n, kind), newbank()
+        mm(ph, [("i1", b, a) for b, a in hi] + ([(const, "one", 0)] if his else []), n, stop=False)
+        pl = newbank()
+        mm(pl, [("i1", b, a) for b, a in lo] + ([(const, "one", 0)] if los else []), n, stop=False)
         mm(ph, [("ik", "tY", o)], n, start=False)
         mm(pl, [("ik", "tB", o)], n, start=False)
         return ph, pl, o
 
+    KC = {"in": "ku", "edge": "ke", "out": "kd"}
+
     def double(lo, hi, n, kind, dh, h0, dl, l0):
-        ph, pl, o = pair(lo, hi, n, kind, {"out": "kd", "in": "ku", "edge": "ke"}[kind])
+        ph, pl, o = pair(lo, hi, n, kind, KC[kind], True, True)
         h0, l0 = (o if h0 is None else h0), (o if l0 is None else l0)
         tt(dh, h0, "tY", o, ph, 0, n, 1, OP.max)
         tt(dl, l0, "tB", o, pl, 0, n, 1, OP.max)
         return o
 
-    def double_a(lo, hi, n, dh, h0, dl, l0):
-        ph, pl, o = pair(lo, hi, n, "out")
-        for u, ps, t, dst, d0 in (("uh", ph, "tY", dh, h0), ("ul", pl, "tB", dl, l0)):
-            act(u, o, ps, 0, n, AF.Relu, 1.0, -128 * 256.0)
-            pf = newbank()
-            mm(pf, [("i1", t, o), ("i1", u, o)], n)
-            act(dst, d0, pf, 0, n)
+    def double_a(lo, hi, n, kind, dh, h0, dl, l0):
+        ph, pl, o = pair(lo, hi, n, kind, KC[kind], True, False)
+        tt(dh, h0, "tY", o, ph, 0, n, 1, OP.max)
+        act("ul", o, pl, 0, n, AF.Relu, 1.0, (-128 if kind == "out" else 128) * 256.0)
+        pf = newbank()
+        mm(pf, [("i1", "tB", o), ("i1", "ul", o)], n)
+        act(dl, l0, pf, 0, n)
 
-    def gather(eng, dst, d0, src, a, b, off, c0, n):
+    def gather(eng, dst, d0, src, a, b, off, c0, n, bias=0.0):
         ind = lambda: T[src][:, a:b].indirect(T[off][:, c0:c0 + n // 16])
         R, W = [(src, a, b), (off, c0, c0 + n // 16)], [(dst, d0, d0 + n)]
-        if eng == "V":
+        if eng == "V" and bias:
+            V(lambda: g.vector.tensor_scalar(T[dst][:, d0:d0 + n], ind(), bias, None, OP.add), n, GA, R, W)
+        elif eng == "V":
             V(lambda: g.vector.tensor_copy(T[dst][:, d0:d0 + n], ind()), n, GA, R, W)
         else:
-            A(lambda: g.scalar.activation(T[dst][:, d0:d0 + n], ind(), AF.Copy), n, GA, R, W)
+            A(lambda: g.scalar.activation(T[dst][:, d0:d0 + n], ind(), AF.Copy, bias=bias), n, GA, R, W)
 
     def silu(win, a, b, off, c0, src, s0, n):
         A(lambda: g.scalar.activation(T[win][:, a:b].indirect(T[off][:, c0:c0 + n // 16]), T[src][:, s0:s0 + n], AF.Silu), n, SC,
@@ -153,7 +160,7 @@ def rank_program(g, core, T, topo):
 
     CA = lambda c: ("Y", 2048 + c) if c < 2048 else ("ca", c - 2048)
     CB = lambda c: ("Y", c) if c < 2048 else ("cb", c - 2048)
-    OO = lambda c: ("X", c) if c < 2048 else ("oo", c - 2048)
+    OO = lambda c: ("X", c) if c < 2048 else ("oo", c - 2048) if c < 3072 else ("X", S[3] - 2048 + c - 3072)
 
     def load(eng, i, dst, a, b, src, lat):
         q = g.sync if eng == "Y" else g.scalar
@@ -166,14 +173,14 @@ def rank_program(g, core, T, topo):
     load("A", 6, "ri", 0, 240, "right", 3000)
     load("Y", 7, "ei", 0, 128, "edge", 6500)
 
-    fill("one", 0, 128, 0, 256, 1.0)
+    fill("one", 0, 128, 0, 512, 1.0)
     G(lambda: g.affine_select(T.i1[:], T.one[:, 0:128], [[-1, 128]], OP.is_equal, 0.0, 0, 1), 128, [("one", 0, 128)], [("i1", 0, 128)])
     for nm in DIAG:
         if nm != "i1":
             ts(nm, 0, "i1", 0, 128, .5, DIAG[nm], OP.mult)
     fill("ku", 0, 128, 0, 128, 255.0)
-    fill("kc", 0, 64, 0, 128, 2.0 ** (PB + 1))
-    fill("kc", 64, 128, 0, 128, 2.0)
+    fill("kc", 0, 64, 0, 128, 2.0 ** (PB + 2))
+    fill("kc", 64, 128, 0, 128, 4.0)
     fill("kd", 0, 64, 0, 128, -512.0)
     fill("kd", 64, 128, 0, 128, -2.0)
     fill("ke", 0, 64, 0, 128, 512.0)
@@ -212,7 +219,7 @@ def rank_program(g, core, T, topo):
         ts("f2", f, "raw", a, 512, .5, .5, OP.mult, 132 - .25, OP.add)
         ts("f4", f, "raw", a, 512, .5, .25, OP.mult, 131 - .375, OP.add)
         ps, terms = newbank(), [("i2", "f2", f), ("i8", "f4", f), ("i32", "f8", f)]
-        if a % 1024:
+        if a not in CONV_A:
             ts("f8", f, "raw", a, 512, .5, 8.0, OP.is_ge, -37.0, OP.add)
             mm(ps, terms, 512)
             tt("win", a, "raw", a, ps, 0, 512, 1, OP.add)
@@ -227,7 +234,7 @@ def rank_program(g, core, T, topo):
     V(lambda: g.vector.memset(T.X[:, S[4] - 2048:S[5] - 2048], 85.0), 256, .5, [], [("X", S[4] - 2048, S[5] - 2048)])
     for a in range(0, 4096, 512):
         ramp("val", a, 512, 1, 4096 + a)
-    ramp("Y", 4096, 16, 0, 0)
+    ramp("Y", 4096, 16, 0, 256)
     for a in range(4096, S[5], 1280):
         ramp("W", a, 1280, 1, 4096 + a)
     G(lambda: g.affine_select(T.i1f[:], T.onef[:], [[-1, 128]], OP.is_equal, 0.0, 0, 1), 128, [("onef", 0, 128)], [("i1f", 0, 128)])
@@ -244,15 +251,14 @@ def rank_program(g, core, T, topo):
         base, nn, n = S[d] - 4096, S[d + 1] - S[d], CHUNK[d]
         for a in range(0, nn, n):
             c, w, h = base + a, S[d] + a, n // 2
-            gather("A", *CA(c), "win", S[d - 1], S[d], "lo", c // 16, n)
-            gather("V" if a % 1024 == 0 or d == 3 else "A", *CB(c), "win", S[d - 1], S[d], "ro", c // 16, n)
-            double([CA(c), CB(c)], [CA(c + h), CB(c + h)], h, "in", "win", w + h, "win", w)
+            bias = -128.0 if d > 2 else 0.0
+            gather(on("l", c), *CA(c), "win", S[d - 1], S[d], "lo", c // 16, n, bias)
+            gather(on("r", c), *CB(c), "win", S[d - 1], S[d], "ro", c // 16, n, bias)
+            double([CA(c), CB(c)], [CA(c + h), CB(c + h)], h, "edge" if d > 2 else "in", "win", w + h, "win", w)
 
-    for k, x, y in ((0, "cb", "lo"), (256, "ca", "ro")):
-        ts("top", k, x, 1536, 256, .5, 85.0 - 128.0, OP.add)
-        V(lambda k=k, y=y: g.vector.tensor_copy(T.X[:, S[3] - 2048:S[4] - 2048].indirect(T[y][:, 224:240]), T.top[:, k:k + 256]), 256, SC,
-          [("top", k, k + 256), (y, 224, 240)], [("X", S[3] - 2048, S[4] - 2048)])
-    ts("oo", 1024, "X", S[3] - 2048, 512, .5, -85.0 - 128.0, OP.add)
+    for x, y in (("cb", "lo"), ("ca", "ro")):
+        V(lambda x=x, y=y: g.vector.tensor_copy(T.X[:, S[3] - 2048:S[4] - 2048].indirect(T[y][:, 224:240]), T[x][:, 1536:1792]), 256, SC,
+          [(x, 1536, 1792), (y, 224, 240)], [("X", S[3] - 2048, S[4] - 2048)])
 
     for q in others + [rank]:
         dst, off = ("land", "cu") if q == rank else ("clout", "cin")
@@ -265,27 +271,25 @@ def rank_program(g, core, T, topo):
     for s in range(16):
         P([lambda s=s, ps=ps: g.tensor.matmul(T[ps][:, 0:128], T.selm[:, 128 * s:128 * s + 128], T.val[:, s:2048:16], s == 0, s == 15)],
           512, [("selm", 128 * s, 128 * s + 128), ("val", 0, 2048)], [(ps, 0, 512)])
-    ts("ej", 0, ps, 0, 128, 1, -4095.75, OP.add)
-    ts("ek", 0, "ej", 0, 128, 1, 2048.0, OP.is_ge, -2048.0, OP.mult)
-    tt("el", 0, "ej", 0, "ek", 0, 128, 2, OP.add)
-    ts("e2", 0, "ej", 0, 128, 1, 4096.0, OP.min)
-    ts("e1", 0, "el", 0, 128, 1)
+    ts("e2", 0, ps, 0, 128, 1, -4095.75, OP.add, 4096.25, OP.min)
+    ts("ek", 0, ps, 0, 128, 1, 6143.5, OP.is_ge, -2048.0, OP.mult)
+    tt("el", 0, "ek", 0, ps, 0, 128, 1, OP.add)
+    ts("e1", 0, "el", 0, 128, 1, -4095.75, OP.add)
 
     for d in (3, 2, 1):
-        base, nn, n, h = S[d] - 4096, S[d + 1] - S[d], 512, 256
+        base, nn, n, h = S[d] - 4096, S[d + 1] - S[d], *((1024, 512) if d == 1 else (512, 256))
         lo_, hi_ = S[d - 1] - 2048, S[d] - 2048
         for a in range(0, nn, n):
             c, w = base + a, S[d] + a - 2048
-            if (d, a) in BY_A:
-                double_a([("X", w)], [("X", w + h)], h, *OO(c + h), *OO(c))
-            elif d < 3:
-                double([("X", w)], [("X", w + h)], h, "out", *OO(c + h), *OO(c))
+            if d < 3:
+                (double_a if (d, a) in BY_A else double)([("X", w)], [("X", w + h)], h, "out" if d == 2 else "edge", *OO(c + h), *OO(c))
             if d > 1:
                 q = c - 2048
+                ob, oa = OO(c)
                 for off, sib in (("lo", "cb"), ("ro", "ca")):
-                    V(lambda off=off, sib=sib, c=c, q=q, n=n, lo_=lo_, hi_=hi_: g.vector.tensor_tensor(
-                        T.X[:, lo_:hi_].indirect(T[off][:, c // 16:(c + n) // 16]), T.oo[:, q:q + n], T[sib][:, q:q + n], OP.add), n, SC,
-                      [("oo", q, q + n), (sib, q, q + n), (off, c // 16, (c + n) // 16)], [("X", lo_, hi_)])
+                    V(lambda off=off, sib=sib, c=c, q=q, n=n, lo_=lo_, hi_=hi_, ob=ob, oa=oa: g.vector.tensor_tensor(
+                        T.X[:, lo_:hi_].indirect(T[off][:, c // 16:(c + n) // 16]), T[ob][:, oa:oa + n], T[sib][:, q:q + n], OP.add), n, SC,
+                      [(ob, oa, oa + n), (sib, q, q + n), (off, c // 16, (c + n) // 16)], [("X", lo_, hi_)])
 
     def sel(d0, s0, src, pat, o, base, cm):
         G(lambda: g.affine_select(T.gsum[:, d0:d0 + 32], T[src][:, s0:s0 + 32], pat, o, 0.0, base, cm), 32, [reg(src, s0, 32)], [("gsum", d0, d0 + 32)])
@@ -300,7 +304,7 @@ def rank_program(g, core, T, topo):
     for a in blocks:
         gather("A", "ine", a, "win", 0, S[5], "eu", a // 16, 512)
     for a in blocks:
-        gather("A", "ye", a, "Y", 0, 4112, "e2", a // 16, 512)
+        gather("A", "ye", a, "Y", 0, 4112, "e2", a // 16, 512, -256.0)
     for a in blocks:
         if a in BY_V:
             V(lambda a=a: g.vector.tensor_tensor(T.ole[:, a:a + 512], T.X[:, 0:S[5] - 2048].indirect(T.e1[:, a // 16:a // 16 + 32]), T.ye[:, a:a + 512], OP.add), 512, GA,
@@ -312,22 +316,25 @@ def rank_program(g, core, T, topo):
         if a in BY_MAX:
             o = double(sum_(a), sum_(a + n), n, "edge", "uh", None, "ul", None)
         else:
-            ph, pl, o = pair(sum_(a), sum_(a + n), n, "edge")
-            act("uh", o, ph, 0, n, AF.Relu, 1.0, 128 * 256.0)
+            ph, pl, o = pair(sum_(a), sum_(a + n), n, "edge", "ke", a not in BY_REL, False)
+            if a in BY_REL:
+                act("uh", o, ph, 0, n, AF.Relu, 1.0, 128 * 256.0)
+            else:
+                tt("uh", o, "tY", o, ph, 0, n, 1, OP.max)
             act("ul", o, pl, 0, n, AF.Relu, 1.0, 128 * 256.0)
         mid[a] = o
     for a in blocks:
         h, o = a + n, mid[a]
-        tl, th = ([], []) if a in BY_MAX else ([("tB", o)], [("tY", o)])
-        ph, pl, o2 = pair([("ine", a), ("ul", o)] + tl, [("ine", h), ("uh", o)] + th, n, "in")
+        tl = [] if a in BY_MAX else [("tB", o)]
+        th = [("tY", o)] if a in BY_REL else []
+        ph, pl, o2 = pair([("ine", a), ("ul", o)] + tl, [("ine", h), ("uh", o)] + th, n, "in", "ku", False, False)
         act("uh", o2, ph, 0, n, AF.Relu, 1.0, 127 * 256.0)
         act("ul", o2, pl, 0, n, AF.Relu, 1.0, 127 * 256.0)
         mid2[a] = o2
     for a in blocks:
         h, o2 = a + n, mid2[a]
-        o = split([("land", a), ("tB", o2), ("ul", o2)], [("land", h), ("tY", o2), ("uh", o2)], n, "in")
+        o = split([("land", a), ("tB", o2), ("ul", o2)], [("land", h), ("uh", o2), ("tY", o2)], n, "test", a)
         act("zz", h, "tY", o, n, AF.Relu, -1.0, 129.0)
-        act("zz", a, "tB", o, n, AF.Relu, -1.0, 129.0)
         ps = newbank()
         fns = []
         for kk in range(2):
@@ -341,7 +348,7 @@ def rank_program(g, core, T, topo):
         P(fns, 64, [("gsum", 0, 128), ("zz", a, a + 512), ("kmat", 0, 256), ("inv", 0, 64)], [(ps, 0, 512)])
         r = a // 4
         if a == 0:
-            V(lambda ps=ps: g.vector.tensor_copy(T.key[:, 0:128], T[ps][0:32, 0:128]), 128, 1, [(ps, 0, 512)], [("key", 0, 128)])
+            A(lambda ps=ps: g.scalar.activation(T.key[:, 0:128], T[ps][0:32, 0:128], AF.Copy), 128, 1, [(ps, 0, 512)], [("key", 0, 128)])
         else:
             V(lambda ps=ps, r=r: g.vector.tensor_tensor(T.key[:, r:r + 128], T.key[:, r - 128:r], T[ps][0:32, 0:128], OP.min), 128, 1,
               [(ps, 0, 512), ("key", r - 128, r)], [("key", r, r + 128)])

from concourse.bass import DstId, RemoteDMATransfer
from concourse.mybir import AluOpType as OP, ActivationFunctionType as AF

S = [0, 4096, 6144, 7168, 7680, 7936]
NT = 12
PB = 14
CHUNK = {1: 512, 2: 256, 3: 256, 4: 256}
GA, SC = 1.56, 3.8
LATE = 12000
BY_A = ((1, 0),)
BY_V = (0, 1024)
BY_MAX = (1024, 1536)
BY_REL = (0,)
CONV_A = (512, 1024, 1536, 3072)
ON_V = (("r", 0), ("r", 1024), ("r", 2048), ("r", 3072), ("r", 3328), ("r", 3584))

BUFS = {
    "bfloat16": {"raw": 4096, "f2": 2048, "f4": 2048, "f8": 2048, "win": 7936, "X": 5888, "Y": 4112, "ca": 1792, "cb": 1792,
                 "oo": 1024, "tY": 256 * NT, "tB": 256 * NT, "uh": 256 * NT, "ul": 256 * NT,
                 "ole": 2048, "ye": 2048, "ine": 2048, "zz": 2048, "land": 2048, "clout": 2048, "one": 512, "gsum": 192,
                 "ku": 128, "kc": 128, "kd": 128, "ke": 128, "kmat": 256, "inv": 64},
    "float32": {"key": 512, "res": 128, "W": 7936, "val": 4096, "ek": 128, "el": 128, "onef": 128, "i1f": 128, "selm": 2048},
    "int32": {"tS": 256 * NT, "tT": 256 * NT, "li": 240, "ri": 240, "ci": 128, "ei": 128, "keyi": 192},
    "uint16": {"lo": 240, "ro": 240, "cu": 128, "cin": 128, "eu": 128, "e1": 128, "e2": 128},
}
DIAG = {"i1": 1.0, "i2": 2.0, "i8": 8.0, "i32": 32.0, "ik": -256.0, "ip": 2.0 ** -PB, "iq": 2.0 ** PB}
SCRATCH = {}
for _t in BUFS:
    for _b in BUFS[_t]:
        SCRATCH[_b] = ("sbuf", [32 if _b in ("key", "keyi", "res") else 128, BUFS[_t][_b]], _t)
for _b in DIAG:
    SCRATCH[_b] = ("sbuf", [128, 128], "bfloat16")
for _b in range(8):
    SCRATCH["ps%d" % _b] = ("psum", [128, 512], "float32")
SEMAPHORES = (["qV", "qA", "qP", "qG", "snd"] + ["ld%d" % i for i in range(10)] + ["lst%d" % i for i in range(4)]
              + ["clr%d" % i for i in range(4)])


def rank_program(g, core, T, topo):
    rank = T.rank_of(core)
    if rank is None:
        return
    others = [q for q in range(len(T.cores)) if q != rank]
    ops = []

    def op(eng, fns, cost, R=(), W=(), lat=0.0, dma=None, inc=0, seen=None):
        ops.append({"eng": eng, "fns": fns, "cost": cost, "R": list(R), "W": list(W), "lat": lat, "dma": dma, "inc": inc, "seen": seen})

    def V(fn, n, c, R, W):
        op("V", [fn], 30 + 1.04 * max(64, n * c), R, W)

    def A(fn, n, c, R, W):
        op("A", [fn], 50 + 1.04 * n * c, R, W)

    def P(fns, n, R, W):
        op("P", fns, 20 + 0.45 * max(64, n) * len(fns), R, W)

    def G(fn, n, R, W):
        op("G", [fn], 150 + 2.08 * n, R, W)

    on = lambda k, a: "V" if (k, a) in ON_V else "A"
    bank, slots = [0], [0]

    def newbank():
        bank[0] += 1
        return "ps%d" % ((bank[0] - 1) % 8)

    def newslot(n):
        a = slots[0] if slots[0] % (256 * NT) + n <= 256 * NT else slots[0] + 256
        slots[0] = a + n
        return a % (256 * NT)

    def reg(b, a, n):
        return (b, 0, 512) if b[:2] == "ps" else (b, a, a + n)

    def mm(ps, terms, n, start=True, stop=True):
        fns = []
        for k, (m, b, a) in enumerate(terms):
            st, sp = start and k == 0, stop and k == len(terms) - 1
            fns.append(lambda m=m, b=b, a=a, st=st, sp=sp: g.tensor.matmul(T[ps][:, 0:n], T[m][:], T[b][:, a:a + n], st, sp))
        P(fns, n, [(m, 0, 128) for m, b, a in terms] + [(b, a, a + n) for m, b, a in terms], [(ps, 0, 512)])

    def ts(dst, d0, src, s0, n, c, s1=None, op0=None, s2=None, op1=None):
        o, i = (lambda: T[dst][:, d0:d0 + n]), (lambda: T[src][:, s0:s0 + n])
        if op0 is None:
            fn = lambda: g.vector.tensor_copy(o(), i())
        elif op1 is None:
            fn = lambda: g.vector.tensor_scalar(o(), i(), s1, None, op0)
        else:
            fn = lambda: g.vector.tensor_scalar(o(), i(), s1, s2, op0, op1)
        V(fn, n, c, [reg(src, s0, n)], [reg(dst, d0, n)])

    def tt(dst, d0, x, x0, y, y0, n, c, o):
        V(lambda: g.vector.tensor_tensor(T[dst][:, d0:d0 + n], T[x][:, x0:x0 + n], T[y][:, y0:y0 + n], o), n, c,
          [reg(x, x0, n), reg(y, y0, n)], [reg(dst, d0, n)])

    def act(dst, d0, src, s0, n, func=AF.Copy, scale=1.0, bias=0.0):
        A(lambda: g.scalar.activation(T[dst][:, d0:d0 + n], T[src][:, s0:s0 + n], func, bias=bias, scale=scale), n, 1,
          [reg(src, s0, n)], [reg(dst, d0, n)])

    def fill(buf, p0, p1, a, b, x):
        V(lambda: g.vector.memset(T[buf][p0:p1, a:b], x), b - a, .5, [], [(buf, a, b)])

    def split(lo, hi, n, kind, z=None):
        pp, o = newbank(), newslot(max(n, 256))
        mm(pp, [("i1", b, a) for b, a in hi] + [("ip", b, a) for b, a in lo], n)
        if kind in ("edge", "out"):
            ts("tS", o, pp, 0, n, 1, 2.0 ** PB, OP.mult, float((256 << PB) + 256), OP.add)
        else:
            ts("tS", o, pp, 0, n, 1, 2.0 ** PB, OP.mult)
        ts("tT", o, "tS", o, n, 1, 1, OP.logical_shift_right, (0x55 if kind == "test" else 0xD5) + (0xD5 << PB), OP.bitwise_and)
        ts("tY", o, "tT", o, n, 1, 2.0 ** -PB, OP.mult, *((-256.0, OP.add) if kind == "out" else ()))
        mm(pp, [("iq", "tY", o)] + ([("kc", "one", 0)] if kind == "out" else []), n)
        if kind == "test":
            tt("zz", z, "tT", o, pp, 0, n, 1, OP.is_equal)
        else:
            tt("tB", o, "tT", o, pp, 0, n, 1, OP.subtract)
        return o

    def pair(lo, hi, n, kind, const, his, los):
        o, ph = split(lo, hi, n, kind), newbank()
        mm(ph, [("i1", b, a) for b, a in hi] + ([(const, "one", 0)] if his else []), n, stop=False)
        pl = newbank()
        mm(pl, [("i1", b, a) for b, a in lo] + ([(const, "one", 0)] if los else []), n, stop=False)
        mm(ph, [("ik", "tY", o)], n, start=False)
        mm(pl, [("ik", "tB", o)], n, start=False)
        return ph, pl, o

    KC = {"in": "ku", "edge": "ke", "out": "kd"}

    def double(lo, hi, n, kind, dh, h0, dl, l0):
        ph, pl, o = pair(lo, hi, n, kind, KC[kind], True, True)
        h0, l0 = (o if h0 is None else h0), (o if l0 is None else l0)
        tt(dh, h0, "tY", o, ph, 0, n, 1, OP.max)
        tt(dl, l0, "tB", o, pl, 0, n, 1, OP.max)
        return o

    def double_a(lo, hi, n, kind, dh, h0, dl, l0):
        ph, pl, o = pair(lo, hi, n, kind, KC[kind], True, False)
        tt(dh, h0, "tY", o, ph, 0, n, 1, OP.max)
        act("ul", o, pl, 0, n, AF.Relu, 1.0, (-128 if kind == "out" else 128) * 256.0)
        pf = newbank()
        mm(pf, [("i1", "tB", o), ("i1", "ul", o)], n)
        act(dl, l0, pf, 0, n)

    def gather(eng, dst, d0, src, a, b, off, c0, n, bias=0.0):
        ind = lambda: T[src][:, a:b].indirect(T[off][:, c0:c0 + n // 16])
        R, W = [(src, a, b), (off, c0, c0 + n // 16)], [(dst, d0, d0 + n)]
        if eng == "V" and bias:
            V(lambda: g.vector.tensor_scalar(T[dst][:, d0:d0 + n], ind(), bias, None, OP.add), n, GA, R, W)
        elif eng == "V":
            V(lambda: g.vector.tensor_copy(T[dst][:, d0:d0 + n], ind()), n, GA, R, W)
        else:
            A(lambda: g.scalar.activation(T[dst][:, d0:d0 + n], ind(), AF.Copy, bias=bias), n, GA, R, W)

    def silu(win, a, b, off, c0, src, s0, n):
        A(lambda: g.scalar.activation(T[win][:, a:b].indirect(T[off][:, c0:c0 + n // 16]), T[src][:, s0:s0 + n], AF.Silu), n, SC,
          [(src, s0, s0 + n), (off, c0, c0 + n // 16)], [(win, a, b)])
        ops[-1]["late"] = LATE

    CA = lambda c: ("Y", 2048 + c) if c < 2048 else ("ca", c - 2048)
    CB = lambda c: ("Y", c) if c < 2048 else ("cb", c - 2048)
    OO = lambda c: ("X", c) if c < 2048 else ("oo", c - 2048) if c < 3072 else ("X", S[3] - 2048 + c - 3072)

    def load(eng, i, dst, a, b, src, lat):
        q = g.sync if eng == "Y" else g.scalar
        op(eng, [lambda: q.dma_start(T[dst][:, a:b], T[src][:, a:b])], 120, [], [(dst, a, b)], lat=lat, dma="ld%d" % i, inc=16)

    for k in range(4):
        load("Y", k, "raw", 1024 * k, 1024 * k + 1024, "leaf", 2000 + 800 * k)
    load("A", 4, "ci", 0, 128, "clade", 2200)
    load("A", 5, "li", 0, 240, "left", 2600)
    load("A", 6, "ri", 0, 240, "right", 3000)
    load("Y", 7, "ei", 0, 128, "edge", 6500)

    fill("one", 0, 128, 0, 512, 1.0)
    G(lambda: g.affine_select(T.i1[:], T.one[:, 0:128], [[-1, 128]], OP.is_equal, 0.0, 0, 1), 128, [("one", 0, 128)], [("i1", 0, 128)])
    for nm in DIAG:
        if nm != "i1":
            ts(nm, 0, "i1", 0, 128, .5, DIAG[nm], OP.mult)
    fill("ku", 0, 128, 0, 128, 255.0)
    fill("kc", 0, 64, 0, 128, 2.0 ** (PB + 2))
    fill("kc", 64, 128, 0, 128, 4.0)
    fill("kd", 0, 64, 0, 128, -512.0)
    fill("kd", 64, 128, 0, 128, -2.0)
    fill("ke", 0, 64, 0, 128, 512.0)
    fill("ke", 64, 128, 0, 128, 2.0)
    fill("onef", 0, 128, 0, 128, 1.0)
    fill("inv", 0, 128, 0, 64, 2.0 ** -7)

    ts("cu", 0, "ci", 0, 128, 1)
    for d in range(1, 5):
        c0, c1 = (S[d] - 4096) // 16, (S[d + 1] - 4096) // 16
        for x, y in (("li", "lo"), ("ri", "ro")):
            ts(y, c0, x, c0, c1 - c0, 1, float(-S[d - 1]), OP.add)

    def fused(src, dst, w, sem):
        tr = []
        for i, q in enumerate(others):
            to = T.cores[q]
            rid, pid, _e = topo.addr(to)
            en = topo.engines(core, to)[4 * i:4 * i + 4]
            tr.append(RemoteDMATransfer(dst_ids=[DstId(rid=rid, pnc=pid)], dma_engine_mask=sum(1 << e for e in en),
                                        remote_sem=T.sem[sem + str(rank)], src=T[src][:, w * q:w * q + w],
                                        dst=T[dst][:, w * rank:w * rank + w]))
        g.remote_dma_fused(tr, local_sem=T.sem.snd)
        return None

    def exchange(src, dst, w, sem, t):
        op("G", [lambda: fused(src, dst, w, sem)], 1500, [(src, w * q, w * q + w) for q in others], [], lat=2000, dma="snd", inc=12)
        for q in others:
            op(None, [], t, [], [(dst, w * q, w * q + w)], seen=(sem + str(q), 4))

    exchange("cu", "cin", 32, "lst", 6000)
    ts("eu", 0, "ei", 0, 128, 1)

    for a in range(0, 4096, 512):
        f = a % 2048
        ts("f2", f, "raw", a, 512, .5, .5, OP.mult, 132 - .25, OP.add)
        ts("f4", f, "raw", a, 512, .5, .25, OP.mult, 131 - .375, OP.add)
        ps, terms = newbank(), [("i2", "f2", f), ("i8", "f4", f), ("i32", "f8", f)]
        if a not in CONV_A:
            ts("f8", f, "raw", a, 512, .5, 8.0, OP.is_ge, -37.0, OP.add)
            mm(ps, terms, 512)
            tt("win", a, "raw", a, ps, 0, 512, 1, OP.add)
        else:
            act("f8", f, "raw", a, 512, AF.Copy, .125, 129 - .4375)
            mm(ps, [("i1", "raw", a)] + terms, 512)
            act("win", a, ps, 0, 512, AF.Copy, 1.0, 128.0 - 32.0 * (129 + 41))

    def ramp(buf, a, n, step, base):
        G(lambda: g.iota(T[buf][:, a:a + n], [[step, n]], base, 0, allow_small_or_imprecise_dtypes=True), n, [("i1", 0, 128)], [(buf, a, a + n)])

    V(lambda: g.vector.memset(T.X[:, S[4] - 2048:S[5] - 2048], 85.0), 256, .5, [], [("X", S[4] - 2048, S[5] - 2048)])
    for a in range(0, 4096, 512):
        ramp("val", a, 512, 1, 4096 + a)
    ramp("Y", 4096, 16, 0, 256)
    for a in range(4096, S[5], 1280):
        ramp("W", a, 1280, 1, 4096 + a)
    G(lambda: g.affine_select(T.i1f[:], T.onef[:], [[-1, 128]], OP.is_equal, 0.0, 0, 1), 128, [("onef", 0, 128)], [("i1f", 0, 128)])
    for s in range(16):
        G(lambda s=s: g.affine_select(T.selm[:, 128 * s:128 * s + 128], T.i1f[:], [[0, 8], [1, 16]], OP.is_equal, 0.0, -s, 0), 128,
          [("i1f", 0, 128)], [("selm", 128 * s, 128 * s + 128)])
    G(lambda: g.iota(T.kmat[:], [[1, 8], [0, 32]], 0, 0, allow_small_or_imprecise_dtypes=True), 256, [], [("kmat", 0, 256)])

    for a in range(0, 2048, 256):
        silu("W", 0, 4096, "lo", a // 16, "val", a, 256)
        silu("W", 0, 4096, "ro", a // 16, "val", 2048 + a, 256)

    for d in range(1, 5):
        base, nn, n = S[d] - 4096, S[d + 1] - S[d], CHUNK[d]
        for a in range(0, nn, n):
            c, w, h = base + a, S[d] + a, n // 2
            bias = -128.0 if d > 2 else 0.0
            gather(on("l", c), *CA(c), "win", S[d - 1], S[d], "lo", c // 16, n, bias)
            gather(on("r", c), *CB(c), "win", S[d - 1], S[d], "ro", c // 16, n, bias)
            double([CA(c), CB(c)], [CA(c + h), CB(c + h)], h, "edge" if d > 2 else "in", "win", w + h, "win", w)

    for x, y in (("cb", "lo"), ("ca", "ro")):
        V(lambda x=x, y=y: g.vector.tensor_copy(T.X[:, S[3] - 2048:S[4] - 2048].indirect(T[y][:, 224:240]), T[x][:, 1536:1792]), 256, SC,
          [(x, 1536, 1792), (y, 224, 240)], [("X", S[3] - 2048, S[4] - 2048)])

    for q in others + [rank]:
        dst, off = ("land", "cu") if q == rank else ("clout", "cin")
        gather("A", dst, 512 * q, "win", 0, S[5], off, 32 * q, 512)
    exchange("clout", "land", 512, "clr", 35000)

    for a in range(0, 2048, 512):
        gather("A", "val", a, "W", 0, S[5], "eu", a // 16, 512)
    ps = newbank()
    for s in range(16):
        P([lambda s=s, ps=ps: g.tensor.matmul(T[ps][:, 0:128], T.selm[:, 128 * s:128 * s + 128], T.val[:, s:2048:16], s == 0, s == 15)],
          512, [("selm", 128 * s, 128 * s + 128), ("val", 0, 2048)], [(ps, 0, 512)])
    ts("e2", 0, ps, 0, 128, 1, -4095.75, OP.add, 4096.25, OP.min)
    ts("ek", 0, ps, 0, 128, 1, 6143.5, OP.is_ge, -2048.0, OP.mult)
    tt("el", 0, "ek", 0, ps, 0, 128, 1, OP.add)
    ts("e1", 0, "el", 0, 128, 1, -4095.75, OP.add)

    for d in (3, 2, 1):
        base, nn, n, h = S[d] - 4096, S[d + 1] - S[d], *((1024, 512) if d == 1 else (512, 256))
        lo_, hi_ = S[d - 1] - 2048, S[d] - 2048
        for a in range(0, nn, n):
            c, w = base + a, S[d] + a - 2048
            if d < 3:
                (double_a if (d, a) in BY_A else double)([("X", w)], [("X", w + h)], h, "out" if d == 2 else "edge", *OO(c + h), *OO(c))
            if d > 1:
                q = c - 2048
                ob, oa = OO(c)
                for off, sib in (("lo", "cb"), ("ro", "ca")):
                    V(lambda off=off, sib=sib, c=c, q=q, n=n, lo_=lo_, hi_=hi_, ob=ob, oa=oa: g.vector.tensor_tensor(
                        T.X[:, lo_:hi_].indirect(T[off][:, c // 16:(c + n) // 16]), T[ob][:, oa:oa + n], T[sib][:, q:q + n], OP.add), n, SC,
                      [(ob, oa, oa + n), (sib, q, q + n), (off, c // 16, (c + n) // 16)], [("X", lo_, hi_)])

    def sel(d0, s0, src, pat, o, base, cm):
        G(lambda: g.affine_select(T.gsum[:, d0:d0 + 32], T[src][:, s0:s0 + 32], pat, o, 0.0, base, cm), 32, [reg(src, s0, 32)], [("gsum", d0, d0 + 32)])

    sel(128, 0, "one", [[-16, 8], [0, 4]], OP.is_ge, 0, 1)
    sel(160, 128, "gsum", [[16, 8], [0, 4]], OP.is_ge, 15, -1)
    ts("gsum", 128, "gsum", 160, 32, 1, 8.0, OP.mult)
    for b in range(4):
        sel(32 * b, 128, "gsum", [[0, 8], [1, 4]], OP.is_equal, -b, 0)

    blocks, n, mid, mid2 = range(0, 2048, 512), 256, {}, {}
    for a in blocks:
        gather("A", "ine", a, "win", 0, S[5], "eu", a // 16, 512)
    for a in blocks:
        gather("A", "ye", a, "Y", 0, 4112, "e2", a // 16, 512, -256.0)
    for a in blocks:
        if a in BY_V:
            V(lambda a=a: g.vector.tensor_tensor(T.ole[:, a:a + 512], T.X[:, 0:S[5] - 2048].indirect(T.e1[:, a // 16:a // 16 + 32]), T.ye[:, a:a + 512], OP.add), 512, GA,
              [("X", 0, S[5] - 2048), ("e1", a // 16, a // 16 + 32), ("ye", a, a + 512)], [("ole", a, a + 512)])
        else:
            gather("A", "ole", a, "X", 0, S[5] - 2048, "e1", a // 16, 512)
    for a in blocks:
        sum_ = lambda x: [("ole", x)] + ([] if a in BY_V else [("ye", x)])
        if a in BY_MAX:
            o = double(sum_(a), sum_(a + n), n, "edge", "uh", None, "ul", None)
        else:
            ph, pl, o = pair(sum_(a), sum_(a + n), n, "edge", "ke", a not in BY_REL, False)
            if a in BY_REL:
                act("uh", o, ph, 0, n, AF.Relu, 1.0, 128 * 256.0)
            else:
                tt("uh", o, "tY", o, ph, 0, n, 1, OP.max)
            act("ul", o, pl, 0, n, AF.Relu, 1.0, 128 * 256.0)
        mid[a] = o
    for a in blocks:
        h, o = a + n, mid[a]
        tl = [] if a in BY_MAX else [("tB", o)]
        th = [("tY", o)] if a in BY_REL else []
        ph, pl, o2 = pair([("ine", a), ("ul", o)] + tl, [("ine", h), ("uh", o)] + th, n, "in", "ku", False, False)
        act("uh", o2, ph, 0, n, AF.Relu, 1.0, 127 * 256.0)
        act("ul", o2, pl, 0, n, AF.Relu, 1.0, 127 * 256.0)
        mid2[a] = o2
    for a in blocks:
        h, o2 = a + n, mid2[a]
        o = split([("land", a), ("tB", o2), ("ul", o2)], [("land", h), ("uh", o2), ("tY", o2)], n, "test", a)
        act("zz", h, "tY", o, n, AF.Relu, -1.0, 129.0)
        ps = newbank()
        fns = []
        for kk in range(2):
            k = a // 256 + kk
            for b in range(4):
                fns.append(lambda kk=kk, b=b, ps=ps, a=a: g.tensor.matmul(
                    T[ps][0:32, 64 * kk:64 * kk + 64], T.gsum[:, 32 * b:32 * b + 32],
                    T.zz[:, a + 256 * kk + 64 * b:a + 256 * kk + 64 * b + 64], b == 0, False))
            fns.append(lambda kk=kk, k=k, ps=ps: g.tensor.matmul(
                T[ps][0:32, 64 * kk:64 * kk + 64], T.kmat[:, 32 * k:32 * k + 32], T.inv[:], False, True))
        P(fns, 64, [("gsum", 0, 128), ("zz", a, a + 512), ("kmat", 0, 256), ("inv", 0, 64)], [(ps, 0, 512)])
        r = a // 4
        if a == 0:
            A(lambda ps=ps: g.scalar.activation(T.key[:, 0:128], T[ps][0:32, 0:128], AF.Copy), 128, 1, [(ps, 0, 512)], [("key", 0, 128)])
        else:
            V(lambda ps=ps, r=r: g.vector.tensor_tensor(T.key[:, r:r + 128], T.key[:, r - 128:r], T[ps][0:32, 0:128], OP.min), 128, 1,
              [(ps, 0, 512), ("key", r - 128, r)], [("key", r, r + 128)])
    tt("keyi", 0, "key", 384, "key", 448, 64, 2, OP.min)
    ts("keyi", 64, "keyi", 0, 64, 1, 3, OP.logical_shift_right)
    ts("keyi", 128, "keyi", 0, 64, 1, 7, OP.bitwise_and)
    ts("res", 0, "keyi", 64, 64, 1)
    ts("res", 64, "keyi", 128, 64, 1)
    op("Y", [lambda: g.sync.dma_start(T.cost[:], T.res[:, 0:64])], 120, [("res", 0, 64)], [], lat=2000, dma="ld8", inc=16)
    op("A", [lambda: g.scalar.dma_start(T["first"][:], T.res[:, 64:128])], 120, [("res", 64, 128)], [], lat=2000, dma="ld9", inc=16)

    run(g, T, ops)


def run(g, T, ops):
    n = len(ops)
    deps = [dict() for _ in ops]
    hist = {}
    for i, o in enumerate(ops):
        for kind, regs in (("R", o["R"]), ("W", o["W"])):
            for r in regs:
                psum = r[0][:2] == "ps"
                for (a, b, j, w) in hist.get(r[0], ()):
                    if j == i or not (a < r[2] and r[1] < b):
                        continue
                    same = ops[j]["eng"] == o["eng"]
                    if not w and kind == "R" and (same or not psum):
                        continue
                    hard = (w and kind == "R") or not same or ops[j]["dma"] is not None or o["eng"] != "P"
                    deps[i][j] = deps[i].get(j, False) or hard
        for r in o["R"]:
            hist.setdefault(r[0], []).append((r[1], r[2], i, False))
        for r in o["W"]:
            h = hist.get(r[0], [])
            hist[r[0]] = [e for e in h if not (r[1] <= e[0] and e[1] <= r[2])] + [(r[1], r[2], i, True)]
    succ = [[] for _ in ops]
    for i in range(n):
        for j in deps[i]:
            succ[j].append(i)
    tail = [0.0] * n
    for i in range(n - 1, -1, -1):
        tail[i] = ops[i]["cost"] + ops[i]["lat"] + max([tail[k] + 80 for k in succ[i]] or [0.0])
    for i in range(n):
        tail[i] -= ops[i].get("late", 0)
    free, fin = {}, [0.0] * n
    need = [len(d) for d in deps]
    ready = [i for i in range(n) if not need[i]]
    est = dict((i, 0.0) for i in ready)
    order = []
    while ready:
        best = min(ready, key=lambda i: max(est[i], free.get(ops[i]["eng"], 0.0) if ops[i]["eng"] else 0.0))
        e = ops[best]["eng"]
        bt = max(est[best], free.get(e, 0.0) if e else 0.0)
        if e:
            cand = [i for i in ready if ops[i]["eng"] == e and max(est[i], free.get(e, 0.0)) <= bt + 60]
            best = max(cand, key=lambda i: (tail[i], -i))
            bt = max(est[best], free.get(e, 0.0))
            free[e] = bt + ops[best]["cost"]
        fin[best] = bt + ops[best]["cost"] + ops[best]["lat"]
        order.append(best)
        ready.remove(best)
        for k in succ[best]:
            need[k] -= 1
            if not need[k]:
                ready.append(k)
                est[k] = max(fin[j] + 80 for j in deps[k])
    queue = {"V": g.vector, "A": g.scalar, "P": g.tensor, "G": g, "Y": g.sync}
    csem = {"V": "qV", "A": "qA", "P": "qP", "G": "qG"}
    total, val = {}, [None] * n
    clock = {e: {} for e in queue}
    snap = [None] * n
    for i in order:
        o = ops[i]
        e = o["eng"]
        if e is None:
            val[i], snap[i] = o["seen"], {}
            total[o["seen"][0]] = o["seen"][1]
            continue
        ck = clock[e]
        todo = sorted([j for j in deps[i] if deps[i][j]], key=lambda j: -fin[j])
        for j in todo:
            s = val[j][0]
            if ck.get(s, 0) >= val[j][1]:
                continue
            same = [x for x in todo if val[x][0] == s]
            v = max(val[x][1] for x in same)
            queue[e].wait_ge(T.sem[s], v)
            for x in same:
                for k2, v2 in snap[x].items():
                    ck[k2] = max(ck.get(k2, 0), v2)
            ck[s] = max(ck.get(s, 0), v)
        s = o["dma"] or csem[e]
        for fn in o["fns"]:
            ins = fn()
            if ins is not None:
                ins.then_inc(T.sem[s], o["inc"] or 1)
            total[s] = total.get(s, 0) + (o["inc"] or 1)
        val[i], snap[i] = (s, total[s]), dict(ck)
    for s in sorted(total):
        if clock["Y"].get(s, 0) < total[s]:
            g.sync.wait_ge(T.sem[s], total[s])
    return fin
